import numpy as np
import ml_dtypes


def mxq(x, axis, fmt="e4m3"):
    dtype, down = {"e4m3": (ml_dtypes.float8_e4m3fn, 7), "e5m2": (ml_dtypes.float8_e5m2, 14)}[fmt]
    v = np.moveaxis(np.asarray(x, np.float32).astype(ml_dtypes.bfloat16).astype(np.float64), axis, -1)
    blocks = v.reshape(v.shape[:-1] + (-1, 32))
    amax = np.abs(blocks).max(-1, keepdims=True)
    byte = np.maximum(np.where(amax > 0, np.frexp(amax)[1] - 1 + 127, 0) - down, 1)
    scale = np.exp2(byte - 127.0)
    codes = (blocks / scale).astype(np.float32).astype(dtype).astype(np.float64)
    return np.moveaxis((codes * scale).reshape(v.shape), -1, axis)


WIDE = False


def mx_kscale(k):
    if not WIDE:
        return np.ones(k)
    levels = np.array([24, -24, 12, -12, 0])
    if k % 512:
        return np.exp2(np.random.permutation(np.resize(levels, k // 32))).repeat(32)
    a = np.empty((k // 512, 16))
    for p in range(k // 512):
        a[p, :8] = np.random.permutation(np.resize(levels, 8))
        for g in range(8):
            far = levels[np.abs(levels - a[p, g]) >= 10]
            a[p, g + 8] = far[np.random.randint(len(far))]
    return np.exp2(a.ravel()).repeat(32)


def f64(x):
    return np.asarray(x).astype(np.float64)


def striped8(idx):
    return np.concatenate([v.reshape(-1, 16).T for v in idx]).astype(np.uint16)


def unstriped8(offs):
    return np.stack([offs[16 * g:16 * g + 16].T.reshape(-1) for g in range(8)]).astype(np.int64)


def planes(y):
    n, m = y.shape
    v = y.astype(np.float32).astype(ml_dtypes.bfloat16).astype(np.float64).reshape(n // 32, 32, m)
    top = np.abs(v).max(1)
    byte = np.clip(np.where(top > 0, np.frexp(top)[1] - 1 + 127 - 7, 1), 1, 254)
    codes = (v * np.exp2(127.0 - byte)[:, None, :]).reshape(n, m).astype(np.float32).astype(ml_dtypes.float8_e4m3fn).view(np.uint8)
    words = codes.reshape(n // 512, 128, 4, m).transpose(0, 1, 3, 2)
    return np.ascontiguousarray(words), np.ascontiguousarray(byte.astype(np.uint8).reshape(n // 512, 16, m))


def gelu(f):
    return 0.5 * f * (1.0 + np.tanh(np.sqrt(2.0 / np.pi) * (f + 0.044715 * f**3)))


K, L, N, T, J = 1024, 512, 512, 2048, 1024


def setup_inputs():
    n = np.random.standard_normal
    s = mx_kscale(K)[:, None]
    s2 = mx_kscale(L)[:, None]
    return {
        "xT": (n((K, T)) * s).astype(np.float32),
        "wgt": np.repeat(np.random.uniform(0.5, 2.0, (8, J)), 16, axis=0).astype(np.float32),
        "wt": (n((K, N)) / np.sqrt(K) / s).astype(np.float32),
        "c": (n((L, J)) * s2).astype(np.float32),
        "wx": (n((L, N)) / np.sqrt(L) / s2).astype(np.float32),
        "b": (0.3 * n(N)).astype(np.float32),
        "offs": striped8(np.stack([np.random.permutation(T)[:J] for _ in range(8)])),
    }


def reference(xT, wgt, wt, c, wx, b, offs):
    idx = unstriped8(offs)
    rows = np.arange(K)
    xg = f64(wgt)[rows // 4 % 128] * f64(xT)[rows[:, None], idx[rows % 512 // 64]]
    xT_ = mxq(xg, 0, "e4m3")
    wt_q_ = mxq(f64(wt), 0, "e4m3")
    wt_r_ = mxq(f64(wt) - wt_q_, 0, "e4m3")
    c_ = mxq(f64(c), 0, "e4m3")
    wx_ = mxq(f64(wx), 0, "e4m3")
    y = wt_q_.T @ xT_ + wt_r_.T @ xT_ + wx_.T @ c_
    out_0 = gelu(y + f64(b)[:, None])
    return (out_0,) + planes(out_0)

@@ -1,0 +1,229 @@
+from contextlib import ExitStack
+
+import concourse.mybir as mybir
+from concourse.masks import make_identity
+
+K, L, N, T, J = 1024, 512, 512, 2048, 1024
+FLOPS = 3221225472
+
+F32 = mybir.dt.float32
+BF16 = mybir.dt.bfloat16
+U32 = mybir.dt.uint32
+I32 = mybir.dt.int32
+U16 = mybir.dt.uint16
+U8 = mybir.dt.uint8
+FP8X4 = mybir.dt.float8_e4m3fn_x4
+ALU = mybir.AluOpType
+GELU = mybir.ActivationFunctionType.Gelu_apprx_tanh
+
+P = 128
+PACK = 4
+KP = P * PACK
+HALF = 512
+CHUNKS = ((0, 512), (512, 256), (768, 128), (896, 128))
+
+
+def tile_list_tier_geluP_kernel(tc, xT, wgt, wt, c, wx, b, offs, out_0, out_1, out_2):
+    nc = tc.nc
+    with ExitStack() as ctx:
+        sb = ctx.enter_context(tc.tile_pool(name="sb", bufs=1))
+        ps = ctx.enter_context(tc.psum_pool(name="ps", bufs=1))
+
+        def mx_tiles(name, width):
+            codes = sb.tile([P, width], U32, name=name + "_codes", align_bytes=64)
+            scales = sb.tile([P, width], U8, name=name + "_scales", align_bytes=64)
+            return codes, scales
+
+        def quantize(dst, col, src):
+            width = src.shape[1] // PACK
+            nc.vector.quantize_mx(out=dst[0][:, col : col + width].bitcast(FP8X4), scales=dst[1][:, col : col + width], in_=src)
+
+        def matmul(out, lhs, lcol, rhs, rcol, start, stop):
+            width = out.shape[1]
+            nc.tensor.matmul_mx(
+                out=out,
+                lhsT=lhs[0][:, lcol : lcol + P].bitcast(FP8X4),
+                lhsT_scale=lhs[1][:, lcol : lcol + P],
+                rhs=rhs[0][:, rcol : rcol + width].bitcast(FP8X4),
+                rhs_scale=rhs[1][:, rcol : rcol + width],
+                start=start,
+                stop=stop,
+            )
+
+        def rows(src, a):
+            return src[KP * a : KP * (a + 1), :].rearrange("(p i) w -> p i w", i=PACK)
+
+        offsets = sb.tile([P, J // 16], U16, name="offsets")
+        nc.sync.dma_start(offsets[:], offs)
+        planes = []
+        for n in range(2 * PACK):
+            planes.append(sb.tile([P, T], F32, name="plane%d" % n))
+        wgt_sb = sb.tile([P, J], F32, name="wgt_sb")
+        wt_raw = [sb.tile([P, PACK, N], F32, name="wt_raw%d" % a, align_bytes=64) for a in range(2)]
+        wx_raw = sb.tile([P, PACK, N], F32, name="wx_raw")
+        c_raw = [sb.tile([P, PACK, HALF], F32, name="c_raw%d" % h) for h in range(2)]
+        bias = sb.tile([P, PACK], F32, name="bias")
+        for i in range(PACK):
+            nc.sync.dma_start(planes[i][:], rows(xT, 0)[:, i, :])
+        nc.sync.dma_start(wgt_sb[:], wgt)
+        for a in range(2):
+            nc.sync.dma_start(wt_raw[a][:], rows(wt, a))
+        nc.sync.dma_start(wx_raw[:], rows(wx, 0))
+        nc.sync.dma_start(c_raw[0][:], rows(c, 0)[:, :, :HALF])
+        for i in range(PACK):
+            nc.sync.dma_start(planes[PACK + i][:], rows(xT, 1)[:, i, :])
+        nc.sync.dma_start(c_raw[1][:], rows(c, 0)[:, :, HALF:])
+        nc.sync.dma_start(bias[:], b.rearrange("(p t) -> p t", t=PACK))
+
+        eye_bf = sb.tile([P, KP * PACK], BF16, name="eye_bf", tag="eye_bf", align_bytes=64)
+        ident = sb.tile([P, P], BF16, name="ident")
+        make_identity(nc, ident[:])
+        nc.vector.memset(eye_bf[:], 0.0)
+        for i in range(PACK):
+            nc.scalar.copy(eye_bf[:].rearrange("p (s m i) -> p s m i", s=PACK, i=PACK)[:, i, :, i], ident[:])
+        eye = mx_tiles("eye", KP)
+        quantize(eye, 0, eye_bf[:])
+
+        def deal_weights(raw, name, tag):
+            w_bf = sb.tile([P, N * PACK], BF16, name=name, tag=tag, align_bytes=64)
+            nc.scalar.copy(
+                w_bf[:].rearrange("p (t m i) -> p m i t", t=PACK, i=PACK),
+                raw[:].rearrange("p i (m t) -> p m i t", t=PACK),
+            )
+            return w_bf
+
+        def weave(engine_copy, dst, src):
+            engine_copy(
+                dst.rearrange("p (g r i) -> p g i r", r=4, i=PACK),
+                src.rearrange("p i (g r) -> p g i r", r=4),
+            )
+
+        def weigh(dst, picked, j0, width):
+            MULT_ENGINE.tensor_tensor(
+                dst.rearrange("p (g r i) -> p g i r", r=4, i=PACK),
+                picked.rearrange("p i (g r) -> p g i r", r=4),
+                wgt_sb[:, j0 : j0 + width].rearrange("p (g r) -> p g r", r=4).unsqueeze(2).to_broadcast([P, width // 4, PACK, 4]),
+                ALU.mult,
+            )
+
+        MULT_ENGINE = nc.vector
+        xg = [mx_tiles("xg%d" % a, J) for a in range(2)]
+
+        picked0 = sb.tile([P, PACK, J], F32, name="picked0")
+        for i in range(PACK):
+            nc.vector.tensor_copy(picked0[:, i, :], planes[i][:].indirect(offsets[:]))
+        xg0_bf = sb.tile([P, J * PACK], BF16, name="xg0_bf", align_bytes=64)
+        for h in range(2):
+            weigh(xg0_bf[:, HALF * PACK * h : HALF * PACK * (h + 1)], picked0[:, :, HALF * h : HALF * (h + 1)], HALF * h, HALF)
+
+        wq = [mx_tiles("wq%d" % a, N) for a in range(2)]
+        wr = [mx_tiles("wr%d" % a, N) for a in range(2)]
+        wq_bf = [deal_weights(wt_raw[a], "wq_bf%d" % a, "w_bf%d" % a) for a in range(2)]
+        for a in range(2):
+            quantize(wq[a], 0, wq_bf[a][:])
+        quantize(xg[0], 0, xg0_bf[:])
+        for a in range(2):
+            wr_bf = sb.tile([P, N * PACK], BF16, name="wr_bf%d" % a, tag="w_bf%d" % a, align_bytes=64)
+            for q in range(4):
+                h, u = q // 2, q % 2
+                back = ps.tile([P, 512], F32, name="back%d_%d" % (a, q), tag="bank%d" % (4 * a + q))
+                for i in range(PACK):
+                    for t2 in range(2):
+                        col = (t2 * PACK + i) * 64
+                        matmul(back[:, col : col + 64], eye, P * i, wq[a], P * (2 * u + t2) + 64 * h, True, True)
+                nc.vector.tensor_tensor(
+                    wr_bf[:].rearrange("p (t m i) -> p m i t", t=PACK, i=PACK)[:, 64 * h : 64 * (h + 1), :, 2 * u : 2 * u + 2],
+                    wt_raw[a][:].rearrange("p i (m t) -> p m i t", t=PACK)[:, 64 * h : 64 * (h + 1), :, 2 * u : 2 * u + 2],
+                    back[:].rearrange("p (t i m) -> p m i t", t=2, i=PACK),
+                    ALU.subtract,
+                )
+            quantize(wr[a], 0, wr_bf[:])
+
+        wxq = mx_tiles("wx", N)
+        wx_bf = deal_weights(wx_raw, "wx_bf", "wx_bf")
+        quantize(wxq, 0, wx_bf[:])
+        cq = mx_tiles("c", J)
+        c_bf = sb.tile([P, J * PACK], BF16, name="c_bf", align_bytes=64)
+        for h in range(2):
+            cols = slice(HALF * PACK * h, HALF * PACK * (h + 1))
+            weave(nc.scalar.copy, c_bf[:, cols], c_raw[h][:])
+            quantize(cq, HALF * h, c_bf[:, cols])
+
+        acc = []
+        first_bank = 0
+        for j0, width in CHUNKS:
+            nb = width * PACK // 512
+            acc.append([ps.tile([P, 512], F32, name="acc%d" % (first_bank + n), tag="bank%d" % (first_bank + n)) for n in range(nb)])
+            first_bank = first_bank + nb
+
+        def passes(ci, pairs, opens, closes):
+            j0, width = CHUNKS[ci]
+            per_bank = 512 // width
+            for n, bank in enumerate(acc[ci]):
+                for s, (lhs, rhs) in enumerate(pairs):
+                    for r in range(per_bank):
+                        t = n * per_bank + r
+                        matmul(bank[:, r * width : (r + 1) * width], lhs, P * t, rhs, j0,
+                               opens and s == 0 and r == 0, closes and s == len(pairs) - 1 and r == per_bank - 1)
+
+        for ci in range(len(CHUNKS)):
+            passes(ci, [(wq[0], xg[0]), (wr[0], xg[0]), (wxq, cq)], True, False)
+
+        yq = mx_tiles("y", J)
+        out_rows = out_0.rearrange("(p t) j -> p t j", t=PACK)
+        out_words = out_1[0].rearrange("p j i -> p (j i)").bitcast(I32)
+
+        def gather_half(h):
+            picked = sb.tile([P, PACK, HALF], F32, name="picked1_%d" % h, tag="picked1")
+            for i in range(PACK):
+                nc.vector.tensor_copy(picked[:, i, :], planes[PACK + i][:].indirect(offsets[:, 32 * h : 32 * (h + 1)]))
+            return picked
+
+        def weigh_chunk(ci, picked):
+            j0, width = CHUNKS[ci]
+            x_bf = sb.tile([P, width * PACK], BF16, name="xg1_bf%d" % ci, align_bytes=64)
+            weigh(x_bf[:], picked[:, :, j0 % HALF : j0 % HALF + width], j0, width)
+            return x_bf
+
+        def finish_sum(ci, x_bf):
+            quantize(xg[1], CHUNKS[ci][0], x_bf[:])
+            passes(ci, [(wq[1], xg[1]), (wr[1], xg[1])], False, True)
+
+        def activate(ci, copy):
+            j0, width = CHUNKS[ci]
+            per_bank = 512 // width
+            y = sb.tile([P, PACK, width], F32, name="y%d" % ci, tag=("wt_raw0" if ci == 0 else "y%d" % ci), align_bytes=64)
+            for t in range(PACK):
+                r = t % per_bank
+                nc.scalar.activation(y[:, t, :], acc[ci][t // per_bank][:, r * width : (r + 1) * width], GELU, bias=bias[:, t : t + 1])
+            nc.sync.dma_start(out_rows[:, :, j0 : j0 + width], y[:])
+            y_bf = sb.tile([P, width * PACK], BF16, name="y_bf%d" % ci, tag=("eye_bf" if ci == 0 else "y_bf%d" % ci), align_bytes=64)
+            weave(copy, y_bf[:], y[:])
+            return y_bf
+
+        def hand_on(ci, y_bf):
+            j0, width = CHUNKS[ci]
+            quantize(yq, j0, y_bf[:])
+            nc.sync.dma_start(out_words[:, j0 : j0 + width], yq[0][:, j0 : j0 + width].bitcast(I32))
+
+        first = gather_half(0)
+        x0 = weigh_chunk(0, first)
+        finish_sum(0, x0)
+        second = gather_half(1)
+        y0 = activate(0, nc.scalar.copy)
+        x1 = weigh_chunk(1, second)
+        x2 = weigh_chunk(2, second)
+        finish_sum(1, x1)
+        x3 = weigh_chunk(3, second)
+        finish_sum(2, x2)
+        finish_sum(3, x3)
+        hand_on(0, y0)
+        y1 = activate(1, nc.vector.tensor_copy)
+        y2 = activate(2, nc.vector.tensor_copy)
+        hand_on(1, y1)
+        y3 = activate(3, nc.vector.tensor_copy)
+        hand_on(2, y2)
+        hand_on(3, y3)
+        for q in range(4):
+            queue = nc.sync if q % 2 == 0 else nc.scalar
+            queue.dma_start(out_2[0, 4 * q : 4 * q + 4, :].bitcast(I32), yq[1][32 * q : 32 * q + 4, :].bitcast(I32))

@@ -20,7 +20,7 @@ P = 128
 PACK = 4
 KP = P * PACK
 HALF = 512
-CHUNKS = ((0, 512), (512, 256), (768, 128), (896, 128))
+CHUNKS = ((0, 256), (256, 256), (512, 256), (768, 256))
 
 
 def tile_list_tier_geluP_kernel(tc, xT, wgt, wt, c, wx, b, offs, out_0, out_1, out_2):
@@ -58,22 +58,30 @@ def tile_list_tier_geluP_kernel(tc, xT, wgt, wt, c, wx, b, offs, out_0, out_1, o
         planes = []
         for n in range(2 * PACK):
             planes.append(sb.tile([P, T], F32, name="plane%d" % n))
-        wgt_sb = sb.tile([P, J], F32, name="wgt_sb")
+        wgt_sb = [sb.tile([P, HALF], F32, name="wgt%d" % h) for h in range(2)]
         wt_raw = [sb.tile([P, PACK, N], F32, name="wt_raw%d" % a, align_bytes=64) for a in range(2)]
-        wx_raw = sb.tile([P, PACK, N], F32, name="wx_raw")
+        wx_raw = sb.tile([P, PACK, N], F32, name="wx_raw", align_bytes=64)
         c_raw = [sb.tile([P, PACK, HALF], F32, name="c_raw%d" % h) for h in range(2)]
         bias = sb.tile([P, PACK], F32, name="bias")
-        for i in range(PACK):
-            nc.sync.dma_start(planes[i][:], rows(xT, 0)[:, i, :])
-        nc.sync.dma_start(wgt_sb[:], wgt)
-        for a in range(2):
-            nc.sync.dma_start(wt_raw[a][:], rows(wt, a))
+
+        def load_plane(n):
+            nc.sync.dma_start(planes[n][:], rows(xT, n // PACK)[:, n % PACK, :])
+
+        nc.sync.dma_start(wt_raw[0][:], rows(wt, 0))
+        load_plane(0)
+        for h in range(2):
+            nc.sync.dma_start(wgt_sb[h][:], wgt[:, HALF * h : HALF * (h + 1)])
+        load_plane(1)
+        nc.sync.dma_start(wt_raw[1][:], rows(wt, 1))
+        load_plane(2)
+        load_plane(3)
         nc.sync.dma_start(wx_raw[:], rows(wx, 0))
-        nc.sync.dma_start(c_raw[0][:], rows(c, 0)[:, :, :HALF])
-        for i in range(PACK):
-            nc.sync.dma_start(planes[PACK + i][:], rows(xT, 1)[:, i, :])
-        nc.sync.dma_start(c_raw[1][:], rows(c, 0)[:, :, HALF:])
         nc.sync.dma_start(bias[:], b.rearrange("(p t) -> p t", t=PACK))
+        for h in range(2):
+            load_plane(4 + h)
+            nc.sync.dma_start(c_raw[h][:], rows(c, 0)[:, :, HALF * h : HALF * (h + 1)])
+        load_plane(6)
+        load_plane(7)
 
         eye_bf = sb.tile([P, KP * PACK], BF16, name="eye_bf", tag="eye_bf", align_bytes=64)
         ident = sb.tile([P, P], BF16, name="ident")
@@ -98,31 +106,24 @@ def tile_list_tier_geluP_kernel(tc, xT, wgt, wt, c, wx, b, offs, out_0, out_1, o
                 src.rearrange("p i (g r) -> p g i r", r=4),
             )
 
-        def weigh(dst, picked, j0, width):
-            MULT_ENGINE.tensor_tensor(
-                dst.rearrange("p (g r i) -> p g i r", r=4, i=PACK),
-                picked.rearrange("p i (g r) -> p g i r", r=4),
-                wgt_sb[:, j0 : j0 + width].rearrange("p (g r) -> p g r", r=4).unsqueeze(2).to_broadcast([P, width // 4, PACK, 4]),
+        def pick(dst, n, j0, width):
+            nc.vector.tensor_tensor(
+                dst,
+                planes[n][:].indirect(offsets[:, j0 // 16 : (j0 + width) // 16]),
+                wgt_sb[j0 // HALF][:, j0 % HALF : j0 % HALF + width],
                 ALU.mult,
             )
 
-        MULT_ENGINE = nc.vector
         xg = [mx_tiles("xg%d" % a, J) for a in range(2)]
-
-        picked0 = sb.tile([P, PACK, J], F32, name="picked0")
-        for i in range(PACK):
-            nc.vector.tensor_copy(picked0[:, i, :], planes[i][:].indirect(offsets[:]))
-        xg0_bf = sb.tile([P, J * PACK], BF16, name="xg0_bf", align_bytes=64)
-        for h in range(2):
-            weigh(xg0_bf[:, HALF * PACK * h : HALF * PACK * (h + 1)], picked0[:, :, HALF * h : HALF * (h + 1)], HALF * h, HALF)
-
         wq = [mx_tiles("wq%d" % a, N) for a in range(2)]
         wr = [mx_tiles("wr%d" % a, N) for a in range(2)]
-        wq_bf = [deal_weights(wt_raw[a], "wq_bf%d" % a, "w_bf%d" % a) for a in range(2)]
-        for a in range(2):
-            quantize(wq[a], 0, wq_bf[a][:])
-        quantize(xg[0], 0, xg0_bf[:])
-        for a in range(2):
+        picked0 = [sb.tile([P, PACK, HALF], F32, name="picked0_%d" % h) for h in range(2)]
+
+        def first_tier(a):
+            w_bf = deal_weights(wt_raw[a], "wq_bf%d" % a, "w_bf%d" % a)
+            quantize(wq[a], 0, w_bf[:])
+
+        def second_tier(a):
             wr_bf = sb.tile([P, N * PACK], BF16, name="wr_bf%d" % a, tag="w_bf%d" % a, align_bytes=64)
             for q in range(4):
                 h, u = q // 2, q % 2
@@ -139,9 +140,27 @@ def tile_list_tier_geluP_kernel(tc, xT, wgt, wt, c, wx, b, offs, out_0, out_1, o
                 )
             quantize(wr[a], 0, wr_bf[:])
 
+        def pick_pass0(i):
+            for h in range(2):
+                pick(picked0[h][:, i, :], i, HALF * h, HALF)
+
+        first_tier(0)
+        pick_pass0(0)
+        pick_pass0(1)
+        second_tier(0)
+        first_tier(1)
+        pick_pass0(2)
+        pick_pass0(3)
+        second_tier(1)
+
         wxq = mx_tiles("wx", N)
         wx_bf = deal_weights(wx_raw, "wx_bf", "wx_bf")
         quantize(wxq, 0, wx_bf[:])
+        xg0_bf = sb.tile([P, J * PACK], BF16, name="xg0_bf", tag="wx_raw", align_bytes=64)
+        for h in range(2):
+            cols = slice(HALF * PACK * h, HALF * PACK * (h + 1))
+            weave(nc.scalar.copy, xg0_bf[:, cols], picked0[h][:])
+            quantize(xg[0], HALF * h, xg0_bf[:, cols])
         cq = mx_tiles("c", J)
         c_bf = sb.tile([P, J * PACK], BF16, name="c_bf", align_bytes=64)
         for h in range(2):
@@ -173,16 +192,14 @@ def tile_list_tier_geluP_kernel(tc, xT, wgt, wt, c, wx, b, offs, out_0, out_1, o
         out_rows = out_0.rearrange("(p t) j -> p t j", t=PACK)
         out_words = out_1[0].rearrange("p j i -> p (j i)").bitcast(I32)
 
-        def gather_half(h):
-            picked = sb.tile([P, PACK, HALF], F32, name="picked1_%d" % h, tag="picked1")
-            for i in range(PACK):
-                nc.vector.tensor_copy(picked[:, i, :], planes[PACK + i][:].indirect(offsets[:, 32 * h : 32 * (h + 1)]))
-            return picked
+        picked1 = [sb.tile([P, PACK, width], F32, name="picked1_%d" % ci) for ci, (j0, width) in enumerate(CHUNKS)]
+        for i in range(PACK):
+            for ci, (j0, width) in enumerate(CHUNKS):
+                pick(picked1[ci][:, i, :], PACK + i, j0, width)
 
-        def weigh_chunk(ci, picked):
-            j0, width = CHUNKS[ci]
-            x_bf = sb.tile([P, width * PACK], BF16, name="xg1_bf%d" % ci, align_bytes=64)
-            weigh(x_bf[:], picked[:, :, j0 % HALF : j0 % HALF + width], j0, width)
+        def weave_chunk(ci, copy):
+            x_bf = sb.tile([P, CHUNKS[ci][1] * PACK], BF16, name="xg1_bf%d" % ci, align_bytes=64)
+            weave(copy, x_bf[:], picked1[ci][:])
             return x_bf
 
         def finish_sum(ci, x_bf):
@@ -192,7 +209,7 @@ def tile_list_tier_geluP_kernel(tc, xT, wgt, wt, c, wx, b, offs, out_0, out_1, o
         def activate(ci, copy):
             j0, width = CHUNKS[ci]
             per_bank = 512 // width
-            y = sb.tile([P, PACK, width], F32, name="y%d" % ci, tag=("wt_raw0" if ci == 0 else "y%d" % ci), align_bytes=64)
+            y = sb.tile([P, PACK, width], F32, name="y%d" % ci, tag=("wt_raw%d" % ci if ci < 2 else "y%d" % ci), align_bytes=64)
             for t in range(PACK):
                 r = t % per_bank
                 nc.scalar.activation(y[:, t, :], acc[ci][t // per_bank][:, r * width : (r + 1) * width], GELU, bias=bias[:, t : t + 1])
@@ -206,24 +223,16 @@ def tile_list_tier_geluP_kernel(tc, xT, wgt, wt, c, wx, b, offs, out_0, out_1, o
             quantize(yq, j0, y_bf[:])
             nc.sync.dma_start(out_words[:, j0 : j0 + width], yq[0][:, j0 : j0 + width].bitcast(I32))
 
-        first = gather_half(0)
-        x0 = weigh_chunk(0, first)
+        x0 = weave_chunk(0, nc.scalar.copy)
+        x1 = weave_chunk(1, nc.scalar.copy)
         finish_sum(0, x0)
-        second = gather_half(1)
-        y0 = activate(0, nc.scalar.copy)
-        x1 = weigh_chunk(1, second)
-        x2 = weigh_chunk(2, second)
+        x2 = weave_chunk(2, nc.vector.tensor_copy)
         finish_sum(1, x1)
-        x3 = weigh_chunk(3, second)
+        x3 = weave_chunk(3, nc.vector.tensor_copy)
         finish_sum(2, x2)
         finish_sum(3, x3)
-        hand_on(0, y0)
-        y1 = activate(1, nc.vector.tensor_copy)
-        y2 = activate(2, nc.vector.tensor_copy)
-        hand_on(1, y1)
-        y3 = activate(3, nc.vector.tensor_copy)
-        hand_on(2, y2)
-        hand_on(3, y3)
+        for ci in range(len(CHUNKS)):
+            hand_on(ci, activate(ci, nc.vector.tensor_copy))
         for q in range(4):
             queue = nc.sync if q % 2 == 0 else nc.scalar
             queue.dma_start(out_2[0, 4 * q : 4 * q + 4, :].bitcast(I32), yq[1][32 * q : 32 * q + 4, :].bitcast(I32))

@@ -20,7 +20,9 @@ P = 128
 PACK = 4
 KP = P * PACK
 HALF = 512
-CHUNKS = ((0, 256), (256, 256), (512, 256), (768, 256))
+BANK = 512
+CHUNKS = ((0, 256), (256, 256), (512, 256), (768, 128), (896, 128))
+C_PIECES = ((0, 512), (512, 512))
 
 
 def tile_list_tier_geluP_kernel(tc, xT, wgt, wt, c, wx, b, offs, out_0, out_1, out_2):
@@ -54,54 +56,57 @@ def tile_list_tier_geluP_kernel(tc, xT, wgt, wt, c, wx, b, offs, out_0, out_1, o
             return src[KP * a : KP * (a + 1), :].rearrange("(p i) w -> p i w", i=PACK)
 
         offsets = sb.tile([P, J // 16], U16, name="offsets")
-        nc.sync.dma_start(offsets[:], offs)
-        planes = []
-        for n in range(2 * PACK):
-            planes.append(sb.tile([P, T], F32, name="plane%d" % n))
+        planes = [sb.tile([P, T], F32, name="plane%d" % n, align_bytes=64) for n in range(2 * PACK)]
         wgt_sb = [sb.tile([P, HALF], F32, name="wgt%d" % h) for h in range(2)]
-        wt_raw = [sb.tile([P, PACK, N], F32, name="wt_raw%d" % a, align_bytes=64) for a in range(2)]
+        wt_raw = [sb.tile([P, PACK, N], F32, name="wt_raw%d" % a) for a in range(2)]
         wx_raw = sb.tile([P, PACK, N], F32, name="wx_raw", align_bytes=64)
-        c_raw = [sb.tile([P, PACK, HALF], F32, name="c_raw%d" % h) for h in range(2)]
+        c_raw = [sb.tile([P, PACK, width], F32, name="c_raw%d" % s) for s, (j0, width) in enumerate(C_PIECES)]
         bias = sb.tile([P, PACK], F32, name="bias")
 
         def load_plane(n):
             nc.sync.dma_start(planes[n][:], rows(xT, n // PACK)[:, n % PACK, :])
 
-        nc.sync.dma_start(wt_raw[0][:], rows(wt, 0))
+        def load_c(s):
+            j0, width = C_PIECES[s]
+            nc.sync.dma_start(c_raw[s][:], rows(c, 0)[:, :, j0 : j0 + width])
+
         load_plane(0)
+        nc.sync.dma_start(offsets[:], offs)
         for h in range(2):
             nc.sync.dma_start(wgt_sb[h][:], wgt[:, HALF * h : HALF * (h + 1)])
         load_plane(1)
-        nc.sync.dma_start(wt_raw[1][:], rows(wt, 1))
+        nc.sync.dma_start(wt_raw[0][:], rows(wt, 0))
         load_plane(2)
+        nc.sync.dma_start(wt_raw[1][:], rows(wt, 1))
         load_plane(3)
         nc.sync.dma_start(wx_raw[:], rows(wx, 0))
-        nc.sync.dma_start(bias[:], b.rearrange("(p t) -> p t", t=PACK))
-        for h in range(2):
-            load_plane(4 + h)
-            nc.sync.dma_start(c_raw[h][:], rows(c, 0)[:, :, HALF * h : HALF * (h + 1)])
+        load_c(0)
+        load_plane(4)
+        load_c(1)
+        load_plane(5)
         load_plane(6)
         load_plane(7)
+        nc.sync.dma_start(bias[:], b.rearrange("(p t) -> p t", t=PACK))
 
-        eye_bf = sb.tile([P, KP * PACK], BF16, name="eye_bf", tag="eye_bf", align_bytes=64)
+        eye_bf = sb.tile([P, KP * PACK], BF16, name="eye_bf", tag="picked0", align_bytes=64)
         ident = sb.tile([P, P], BF16, name="ident")
         make_identity(nc, ident[:])
-        nc.vector.memset(eye_bf[:], 0.0)
+        nc.vector.memset(eye_bf[:].bitcast(U32), 0)
         for i in range(PACK):
-            nc.scalar.copy(eye_bf[:].rearrange("p (s m i) -> p s m i", s=PACK, i=PACK)[:, i, :, i], ident[:])
+            nc.vector.tensor_copy(eye_bf[:].rearrange("p (s m i) -> p s m i", s=PACK, i=PACK)[:, i, :, i], ident[:])
         eye = mx_tiles("eye", KP)
         quantize(eye, 0, eye_bf[:])
 
-        def deal_weights(raw, name, tag):
-            w_bf = sb.tile([P, N * PACK], BF16, name=name, tag=tag, align_bytes=64)
-            nc.scalar.copy(
+        def deal_weights(copy, raw, name):
+            w_bf = sb.tile([P, N * PACK], BF16, name=name, align_bytes=64)
+            copy(
                 w_bf[:].rearrange("p (t m i) -> p m i t", t=PACK, i=PACK),
                 raw[:].rearrange("p i (m t) -> p m i t", t=PACK),
             )
             return w_bf
 
-        def weave(engine_copy, dst, src):
-            engine_copy(
+        def weave(copy, dst, src):
+            copy(
                 dst.rearrange("p (g r i) -> p g i r", r=4, i=PACK),
                 src.rearrange("p i (g r) -> p g i r", r=4),
             )
@@ -117,17 +122,24 @@ def tile_list_tier_geluP_kernel(tc, xT, wgt, wt, c, wx, b, offs, out_0, out_1, o
         xg = [mx_tiles("xg%d" % a, J) for a in range(2)]
         wq = [mx_tiles("wq%d" % a, N) for a in range(2)]
         wr = [mx_tiles("wr%d" % a, N) for a in range(2)]
-        picked0 = [sb.tile([P, PACK, HALF], F32, name="picked0_%d" % h) for h in range(2)]
+        picked0_both = sb.tile([P, PACK * J], F32, name="picked0", align_bytes=64)
+        picked0 = [picked0_both[:, PACK * HALF * h : PACK * HALF * (h + 1)].rearrange("p (i w) -> p i w", i=PACK) for h in range(2)]
 
-        def first_tier(a):
-            w_bf = deal_weights(wt_raw[a], "wq_bf%d" % a, "w_bf%d" % a)
-            quantize(wq[a], 0, w_bf[:])
+        def first_tier(a, copy, parts):
+            w_bf = sb.tile([P, N * PACK], BF16, name="wq_bf%d" % a, align_bytes=64)
+            per = PACK // parts
+            for u in range(parts):
+                copy(
+                    w_bf[:].rearrange("p (t m i) -> p m i t", t=PACK, i=PACK)[:, :, :, per * u : per * (u + 1)],
+                    wt_raw[a][:].rearrange("p i (m t) -> p m i t", t=PACK)[:, :, :, per * u : per * (u + 1)],
+                )
+                quantize(wq[a], P * per * u, w_bf[:, KP * per * u : KP * per * (u + 1)])
 
         def second_tier(a):
-            wr_bf = sb.tile([P, N * PACK], BF16, name="wr_bf%d" % a, tag="w_bf%d" % a, align_bytes=64)
+            wr_bf = sb.tile([P, N * PACK], BF16, name="wr_bf%d" % a, tag="plane%d" % (2 + a), align_bytes=64)
             for q in range(4):
-                h, u = q // 2, q % 2
-                back = ps.tile([P, 512], F32, name="back%d_%d" % (a, q), tag="bank%d" % (4 * a + q))
+                u, h = q // 2, q % 2
+                back = ps.tile([P, BANK], F32, name="back%d_%d" % (a, q), tag="bank%d" % (4 * a + q))
                 for i in range(PACK):
                     for t2 in range(2):
                         col = (t2 * PACK + i) * 64
@@ -138,46 +150,53 @@ def tile_list_tier_geluP_kernel(tc, xT, wgt, wt, c, wx, b, offs, out_0, out_1, o
                     back[:].rearrange("p (t i m) -> p m i t", t=2, i=PACK),
                     ALU.subtract,
                 )
-            quantize(wr[a], 0, wr_bf[:])
+            return wr_bf
 
         def pick_pass0(i):
             for h in range(2):
                 pick(picked0[h][:, i, :], i, HALF * h, HALF)
 
-        first_tier(0)
         pick_pass0(0)
         pick_pass0(1)
-        second_tier(0)
-        first_tier(1)
+        first_tier(0, nc.vector.tensor_copy, 1)
         pick_pass0(2)
+        wr_bf0 = second_tier(0)
+        first_tier(1, nc.scalar.copy, 2)
         pick_pass0(3)
-        second_tier(1)
+        quantize(wr[0], 0, wr_bf0[:])
+        wr_bf1 = second_tier(1)
 
         wxq = mx_tiles("wx", N)
-        wx_bf = deal_weights(wx_raw, "wx_bf", "wx_bf")
+        wx_bf = deal_weights(nc.scalar.copy, wx_raw, "wx_bf")
         quantize(wxq, 0, wx_bf[:])
+        quantize(wr[1], 0, wr_bf1[:])
         xg0_bf = sb.tile([P, J * PACK], BF16, name="xg0_bf", tag="wx_raw", align_bytes=64)
         for h in range(2):
             cols = slice(HALF * PACK * h, HALF * PACK * (h + 1))
-            weave(nc.scalar.copy, xg0_bf[:, cols], picked0[h][:])
+            weave(nc.scalar.copy, xg0_bf[:, cols], picked0[h])
             quantize(xg[0], HALF * h, xg0_bf[:, cols])
         cq = mx_tiles("c", J)
         c_bf = sb.tile([P, J * PACK], BF16, name="c_bf", align_bytes=64)
-        for h in range(2):
-            cols = slice(HALF * PACK * h, HALF * PACK * (h + 1))
-            weave(nc.scalar.copy, c_bf[:, cols], c_raw[h][:])
-            quantize(cq, HALF * h, c_bf[:, cols])
+
+        def quantize_c(s):
+            j0, width = C_PIECES[s]
+            cols = slice(PACK * j0, PACK * (j0 + width))
+            weave(nc.scalar.copy, c_bf[:, cols], c_raw[s][:])
+            quantize(cq, j0, c_bf[:, cols])
+
+        quantize_c(0)
+        quantize_c(1)
 
         acc = []
         first_bank = 0
         for j0, width in CHUNKS:
-            nb = width * PACK // 512
-            acc.append([ps.tile([P, 512], F32, name="acc%d" % (first_bank + n), tag="bank%d" % (first_bank + n)) for n in range(nb)])
+            nb = width * PACK // BANK
+            acc.append([ps.tile([P, BANK], F32, name="acc%d" % (first_bank + n), tag="bank%d" % (first_bank + n)) for n in range(nb)])
             first_bank = first_bank + nb
 
         def passes(ci, pairs, opens, closes):
             j0, width = CHUNKS[ci]
-            per_bank = 512 // width
+            per_bank = BANK // width
             for n, bank in enumerate(acc[ci]):
                 for s, (lhs, rhs) in enumerate(pairs):
                     for r in range(per_bank):
@@ -192,14 +211,18 @@ def tile_list_tier_geluP_kernel(tc, xT, wgt, wt, c, wx, b, offs, out_0, out_1, o
         out_rows = out_0.rearrange("(p t) j -> p t j", t=PACK)
         out_words = out_1[0].rearrange("p j i -> p (j i)").bitcast(I32)
 
-        picked1 = [sb.tile([P, PACK, width], F32, name="picked1_%d" % ci) for ci, (j0, width) in enumerate(CHUNKS)]
-        for i in range(PACK):
-            for ci, (j0, width) in enumerate(CHUNKS):
-                pick(picked1[ci][:, i, :], PACK + i, j0, width)
+        def staged(tile, ci):
+            j0, width = CHUNKS[ci]
+            at = PACK * (j0 % HALF)
+            return tile[:, at : at + PACK * width].rearrange("p (i w) -> p i w", i=PACK)
 
-        def weave_chunk(ci, copy):
+        def pick_chunk(tile, ci, i):
+            j0, width = CHUNKS[ci]
+            pick(staged(tile, ci)[:, i, :], PACK + i, j0, width)
+
+        def weave_chunk(tile, ci, copy):
             x_bf = sb.tile([P, CHUNKS[ci][1] * PACK], BF16, name="xg1_bf%d" % ci, align_bytes=64)
-            weave(copy, x_bf[:], picked1[ci][:])
+            weave(copy, x_bf[:], staged(tile, ci))
             return x_bf
 
         def finish_sum(ci, x_bf):
@@ -208,13 +231,13 @@ def tile_list_tier_geluP_kernel(tc, xT, wgt, wt, c, wx, b, offs, out_0, out_1, o
 
         def activate(ci, copy):
             j0, width = CHUNKS[ci]
-            per_bank = 512 // width
-            y = sb.tile([P, PACK, width], F32, name="y%d" % ci, tag=("wt_raw%d" % ci if ci < 2 else "y%d" % ci), align_bytes=64)
+            per_bank = BANK // width
+            y = sb.tile([P, PACK, width], F32, name="y%d" % ci, tag=("wt_raw%d" % ci if ci < 2 else "y%d" % ci))
             for t in range(PACK):
                 r = t % per_bank
                 nc.scalar.activation(y[:, t, :], acc[ci][t // per_bank][:, r * width : (r + 1) * width], GELU, bias=bias[:, t : t + 1])
             nc.sync.dma_start(out_rows[:, :, j0 : j0 + width], y[:])
-            y_bf = sb.tile([P, width * PACK], BF16, name="y_bf%d" % ci, tag=("eye_bf" if ci == 0 else "y_bf%d" % ci), align_bytes=64)
+            y_bf = sb.tile([P, width * PACK], BF16, name="y_bf%d" % ci, align_bytes=64)
             weave(copy, y_bf[:], y[:])
             return y_bf
 
@@ -223,16 +246,25 @@ def tile_list_tier_geluP_kernel(tc, xT, wgt, wt, c, wx, b, offs, out_0, out_1, o
             quantize(yq, j0, y_bf[:])
             nc.sync.dma_start(out_words[:, j0 : j0 + width], yq[0][:, j0 : j0 + width].bitcast(I32))
 
-        x0 = weave_chunk(0, nc.scalar.copy)
-        x1 = weave_chunk(1, nc.scalar.copy)
+        early = sb.tile([P, PACK * HALF], F32, name="early")
+        for i in range(PACK):
+            for ci in range(2):
+                pick_chunk(early, ci, i)
+        x0 = weave_chunk(early, 0, nc.scalar.copy)
+        x1 = weave_chunk(early, 1, nc.scalar.copy)
         finish_sum(0, x0)
-        x2 = weave_chunk(2, nc.vector.tensor_copy)
         finish_sum(1, x1)
-        x3 = weave_chunk(3, nc.vector.tensor_copy)
-        finish_sum(2, x2)
-        finish_sum(3, x3)
+        late = sb.tile([P, PACK * HALF], F32, name="late", tag="wgt0")
+        woven = None
+        for ci in range(2, 5):
+            for i in range(PACK):
+                pick_chunk(late, ci, i)
+            if woven is not None:
+                finish_sum(ci - 1, woven)
+            woven = weave_chunk(late, ci, nc.vector.tensor_copy)
+        finish_sum(4, woven)
         for ci in range(len(CHUNKS)):
-            hand_on(ci, activate(ci, nc.vector.tensor_copy))
+            hand_on(ci, activate(ci, nc.scalar.copy if ci < 2 else nc.vector.tensor_copy))
         for q in range(4):
             queue = nc.sync if q % 2 == 0 else nc.scalar
             queue.dma_start(out_2[0, 4 * q : 4 * q + 4, :].bitcast(I32), yq[1][32 * q : 32 * q + 4, :].bitcast(I32))

@@ -22,6 +22,7 @@ KP = P * PACK
 HALF = 512
 BANK = 512
 CHUNKS = ((0, 256), (256, 256), (512, 256), (768, 128), (896, 128))
+QUARTER = 256
 C_PIECES = ((0, 512), (512, 512))
 
 
@@ -31,8 +32,8 @@ def tile_list_tier_geluP_kernel(tc, xT, wgt, wt, c, wx, b, offs, out_0, out_1, o
         sb = ctx.enter_context(tc.tile_pool(name="sb", bufs=1))
         ps = ctx.enter_context(tc.psum_pool(name="ps", bufs=1))
 
-        def mx_tiles(name, width):
-            codes = sb.tile([P, width], U32, name=name + "_codes", align_bytes=64)
+        def mx_tiles(name, width, tag=""):
+            codes = sb.tile([P, width], U32, name=name + "_codes", tag=tag or name + "_codes", align_bytes=64)
             scales = sb.tile([P, width], U8, name=name + "_scales", align_bytes=64)
             return codes, scales
 
@@ -57,7 +58,7 @@ def tile_list_tier_geluP_kernel(tc, xT, wgt, wt, c, wx, b, offs, out_0, out_1, o
 
         offsets = sb.tile([P, J // 16], U16, name="offsets")
         planes = [sb.tile([P, T], F32, name="plane%d" % n, align_bytes=64) for n in range(2 * PACK)]
-        wgt_sb = [sb.tile([P, HALF], F32, name="wgt%d" % h) for h in range(2)]
+        wgt_sb = [sb.tile([P, HALF], F32, name="wgt%d" % h, align_bytes=64) for h in range(2)]
         wt_raw = [sb.tile([P, PACK, N], F32, name="wt_raw%d" % a) for a in range(2)]
         wx_raw = sb.tile([P, PACK, N], F32, name="wx_raw", align_bytes=64)
         c_raw = [sb.tile([P, PACK, width], F32, name="c_raw%d" % s) for s, (j0, width) in enumerate(C_PIECES)]
@@ -65,10 +66,6 @@ def tile_list_tier_geluP_kernel(tc, xT, wgt, wt, c, wx, b, offs, out_0, out_1, o
 
         def load_plane(n):
             nc.sync.dma_start(planes[n][:], rows(xT, n // PACK)[:, n % PACK, :])
-
-        def load_c(s):
-            j0, width = C_PIECES[s]
-            nc.sync.dma_start(c_raw[s][:], rows(c, 0)[:, :, j0 : j0 + width])
 
         load_plane(0)
         nc.sync.dma_start(offsets[:], offs)
@@ -80,10 +77,9 @@ def tile_list_tier_geluP_kernel(tc, xT, wgt, wt, c, wx, b, offs, out_0, out_1, o
         nc.sync.dma_start(wt_raw[1][:], rows(wt, 1))
         load_plane(3)
         nc.sync.dma_start(wx_raw[:], rows(wx, 0))
-        load_c(0)
-        load_plane(4)
-        load_c(1)
-        load_plane(5)
+        for s, (j0, width) in enumerate(C_PIECES):
+            nc.sync.dma_start(c_raw[s][:], rows(c, 0)[:, :, j0 : j0 + width])
+            load_plane(PACK + s)
         load_plane(6)
         load_plane(7)
         nc.sync.dma_start(bias[:], b.rearrange("(p t) -> p t", t=PACK))
@@ -174,18 +170,12 @@ def tile_list_tier_geluP_kernel(tc, xT, wgt, wt, c, wx, b, offs, out_0, out_1, o
         for h in range(2):
             cols = slice(HALF * PACK * h, HALF * PACK * (h + 1))
             weave(nc.scalar.copy, xg0_bf[:, cols], picked0[h])
-            quantize(xg[0], HALF * h, xg0_bf[:, cols])
-        cq = mx_tiles("c", J)
+        quantize(xg[0], 0, xg0_bf[:])
         c_bf = sb.tile([P, J * PACK], BF16, name="c_bf", align_bytes=64)
-
-        def quantize_c(s):
-            j0, width = C_PIECES[s]
-            cols = slice(PACK * j0, PACK * (j0 + width))
-            weave(nc.scalar.copy, c_bf[:, cols], c_raw[s][:])
-            quantize(cq, j0, c_bf[:, cols])
-
-        quantize_c(0)
-        quantize_c(1)
+        for s in range(2):
+            weave(nc.scalar.copy, c_bf[:, PACK * HALF * s : PACK * HALF * (s + 1)], c_raw[s][:])
+        cq0 = mx_tiles("c0", HALF)
+        quantize(cq0, 0, c_bf[:, : PACK * HALF])
 
         acc = []
         first_bank = 0
@@ -198,14 +188,16 @@ def tile_list_tier_geluP_kernel(tc, xT, wgt, wt, c, wx, b, offs, out_0, out_1, o
             j0, width = CHUNKS[ci]
             per_bank = BANK // width
             for n, bank in enumerate(acc[ci]):
-                for s, (lhs, rhs) in enumerate(pairs):
+                for s, (lhs, rhs, first_col) in enumerate(pairs):
                     for r in range(per_bank):
                         t = n * per_bank + r
-                        matmul(bank[:, r * width : (r + 1) * width], lhs, P * t, rhs, j0,
+                        matmul(bank[:, r * width : (r + 1) * width], lhs, P * t, rhs, j0 - first_col,
                                opens and s == 0 and r == 0, closes and s == len(pairs) - 1 and r == per_bank - 1)
 
         for ci in range(len(CHUNKS)):
-            passes(ci, [(wq[0], xg[0]), (wr[0], xg[0]), (wxq, cq)], True, False)
+            passes(ci, [(wq[0], xg[0], 0), (wr[0], xg[0], 0)], True, False)
+        for ci in range(2):
+            passes(ci, [(wxq, cq0, 0)], False, False)
 
         yq = mx_tiles("y", J)
         out_rows = out_0.rearrange("(p t) j -> p t j", t=PACK)
@@ -213,7 +205,7 @@ def tile_list_tier_geluP_kernel(tc, xT, wgt, wt, c, wx, b, offs, out_0, out_1, o
 
         def staged(tile, ci):
             j0, width = CHUNKS[ci]
-            at = PACK * (j0 % HALF)
+            at = PACK * (j0 - HALF) if j0 >= HALF else 0
             return tile[:, at : at + PACK * width].rearrange("p (i w) -> p i w", i=PACK)
 
         def pick_chunk(tile, ci, i):
@@ -227,34 +219,41 @@ def tile_list_tier_geluP_kernel(tc, xT, wgt, wt, c, wx, b, offs, out_0, out_1, o
 
         def finish_sum(ci, x_bf):
             quantize(xg[1], CHUNKS[ci][0], x_bf[:])
-            passes(ci, [(wq[1], xg[1]), (wr[1], xg[1])], False, True)
+            passes(ci, [(wq[1], xg[1], 0), (wr[1], xg[1], 0)], False, True)
 
-        def activate(ci, copy):
-            j0, width = CHUNKS[ci]
-            per_bank = BANK // width
-            y = sb.tile([P, PACK, width], F32, name="y%d" % ci, tag=("wt_raw%d" % ci if ci < 2 else "y%d" % ci))
-            for t in range(PACK):
-                r = t % per_bank
-                nc.scalar.activation(y[:, t, :], acc[ci][t // per_bank][:, r * width : (r + 1) * width], GELU, bias=bias[:, t : t + 1])
-            nc.sync.dma_start(out_rows[:, :, j0 : j0 + width], y[:])
-            y_bf = sb.tile([P, width * PACK], BF16, name="y_bf%d" % ci, align_bytes=64)
-            weave(copy, y_bf[:], y[:])
-            return y_bf
+        y_bf = sb.tile([P, J * PACK], BF16, name="y_bf", align_bytes=64)
 
-        def hand_on(ci, y_bf):
-            j0, width = CHUNKS[ci]
-            quantize(yq, j0, y_bf[:])
-            nc.sync.dma_start(out_words[:, j0 : j0 + width], yq[0][:, j0 : j0 + width].bitcast(I32))
+        def activate(piece, chunks, copy):
+            j0 = QUARTER * piece
+            y = sb.tile([P, PACK, QUARTER], F32, name="y%d" % piece, tag=("wt_raw%d" % piece if piece < 2 else "y%d" % piece))
+            for ci in chunks:
+                at, width = CHUNKS[ci][0] - j0, CHUNKS[ci][1]
+                per_bank = BANK // width
+                for t in range(PACK):
+                    r = t % per_bank
+                    nc.scalar.activation(
+                        y[:, t, at : at + width], acc[ci][t // per_bank][:, r * width : (r + 1) * width], GELU, bias=bias[:, t : t + 1]
+                    )
+            nc.sync.dma_start(out_rows[:, :, j0 : j0 + QUARTER], y[:])
+            weave(copy, y_bf[:, PACK * j0 : PACK * (j0 + QUARTER)], y[:])
 
-        early = sb.tile([P, PACK * HALF], F32, name="early")
+        def quantize_y(j0, j1):
+            quantize(yq, j0, y_bf[:, PACK * j0 : PACK * j1])
+
+        def store_words(j0, j1):
+            nc.sync.dma_start(out_words[:, j0:j1], yq[0][:, j0:j1].bitcast(I32))
+
+        early = [sb.tile([P, PACK * CHUNKS[ci][1]], F32, name="early%d" % ci) for ci in range(2)]
         for i in range(PACK):
             for ci in range(2):
-                pick_chunk(early, ci, i)
-        x0 = weave_chunk(early, 0, nc.scalar.copy)
-        x1 = weave_chunk(early, 1, nc.scalar.copy)
-        finish_sum(0, x0)
-        finish_sum(1, x1)
-        late = sb.tile([P, PACK * HALF], F32, name="late", tag="wgt0")
+                pick_chunk(early[ci], ci, i)
+        for ci in range(2):
+            finish_sum(ci, weave_chunk(early[ci], ci, nc.scalar.copy))
+        cq1 = mx_tiles("c1", HALF, tag="wgt0")
+        quantize(cq1, 0, c_bf[:, PACK * HALF :])
+        for ci in range(2, 5):
+            passes(ci, [(wxq, cq1, HALF)], False, False)
+        late = sb.tile([P, PACK * HALF], F32, name="late", tag="early0")
         woven = None
         for ci in range(2, 5):
             for i in range(PACK):
@@ -263,8 +262,15 @@ def tile_list_tier_geluP_kernel(tc, xT, wgt, wt, c, wx, b, offs, out_0, out_1, o
                 finish_sum(ci - 1, woven)
             woven = weave_chunk(late, ci, nc.vector.tensor_copy)
         finish_sum(4, woven)
-        for ci in range(len(CHUNKS)):
-            hand_on(ci, activate(ci, nc.scalar.copy if ci < 2 else nc.vector.tensor_copy))
+        activate(0, [0], nc.scalar.copy)
+        activate(1, [1], nc.vector.tensor_copy)
+        quantize_y(0, 256)
+        activate(2, [2], nc.vector.tensor_copy)
+        quantize_y(256, 768)
+        store_words(0, 768)
+        activate(3, [3, 4], nc.scalar.copy)
+        quantize_y(768, J)
+        store_words(768, J)
         for q in range(4):
             queue = nc.sync if q % 2 == 0 else nc.scalar
             queue.dma_start(out_2[0, 4 * q : 4 * q + 4, :].bitcast(I32), yq[1][32 * q : 32 * q + 4, :].bitcast(I32))

@@ -21,9 +21,8 @@ PACK = 4
 KP = P * PACK
 HALF = 512
 BANK = 512
-CHUNKS = ((0, 256), (256, 256), (512, 256), (768, 128), (896, 128))
-QUARTER = 256
-C_PIECES = ((0, 512), (512, 512))
+FIRST = 256
+CHUNKS = ((0, 128), (128, 256), (384, 256), (640, 256), (896, 128))
 
 
 def tile_list_tier_geluP_kernel(tc, xT, wgt, wt, c, wx, b, offs, out_0, out_1, out_2):
@@ -32,8 +31,8 @@ def tile_list_tier_geluP_kernel(tc, xT, wgt, wt, c, wx, b, offs, out_0, out_1, o
         sb = ctx.enter_context(tc.tile_pool(name="sb", bufs=1))
         ps = ctx.enter_context(tc.psum_pool(name="ps", bufs=1))
 
-        def mx_tiles(name, width, tag=""):
-            codes = sb.tile([P, width], U32, name=name + "_codes", tag=tag or name + "_codes", align_bytes=64)
+        def mx_tiles(name, width):
+            codes = sb.tile([P, width], U32, name=name + "_codes", align_bytes=64)
             scales = sb.tile([P, width], U8, name=name + "_scales", align_bytes=64)
             return codes, scales
 
@@ -58,48 +57,64 @@ def tile_list_tier_geluP_kernel(tc, xT, wgt, wt, c, wx, b, offs, out_0, out_1, o
 
         offsets = sb.tile([P, J // 16], U16, name="offsets")
         planes = [sb.tile([P, T], F32, name="plane%d" % n, align_bytes=64) for n in range(2 * PACK)]
-        wgt_sb = [sb.tile([P, HALF], F32, name="wgt%d" % h, align_bytes=64) for h in range(2)]
-        wt_raw = [sb.tile([P, PACK, N], F32, name="wt_raw%d" % a) for a in range(2)]
+        wgt_sb = sb.tile([P, J], F32, name="wgt", align_bytes=64)
+        picked = [sb.tile([P, PACK * J], F32, name="picked%d" % a, tag=("picked0", "plane2")[a], align_bytes=64) for a in range(2)]
+
+        def staged(at, words):
+            return picked[at // (PACK * J)][:, at % (PACK * J) : at % (PACK * J) + words]
+
+        def staged_bf(at, words):
+            return staged(at, words).bitcast(BF16)
+
+        wt_raw = [sb.tile([P, PACK, N], F32, name="wt_raw%d" % a, align_bytes=64)[:] for a in range(2)]
         wx_raw = sb.tile([P, PACK, N], F32, name="wx_raw", align_bytes=64)
-        c_raw = [sb.tile([P, PACK, width], F32, name="c_raw%d" % s) for s, (j0, width) in enumerate(C_PIECES)]
+        c_raw = [sb.tile([P, PACK, HALF], F32, name="c_raw%d" % s) for s in range(2)]
         bias = sb.tile([P, PACK], F32, name="bias")
 
         def load_plane(n):
             nc.sync.dma_start(planes[n][:], rows(xT, n // PACK)[:, n % PACK, :])
 
-        load_plane(0)
+        def load_c(s):
+            nc.sync.dma_start(c_raw[s][:], rows(c, 0)[:, :, HALF * s : HALF * (s + 1)])
+
         nc.sync.dma_start(offsets[:], offs)
-        for h in range(2):
-            nc.sync.dma_start(wgt_sb[h][:], wgt[:, HALF * h : HALF * (h + 1)])
+        nc.sync.dma_start(wgt_sb[:, :FIRST], wgt[:, :FIRST])
+        load_plane(0)
+        nc.sync.dma_start(wgt_sb[:, FIRST:], wgt[:, FIRST:])
         load_plane(1)
-        nc.sync.dma_start(wt_raw[0][:], rows(wt, 0))
         load_plane(2)
-        nc.sync.dma_start(wt_raw[1][:], rows(wt, 1))
         load_plane(3)
+        nc.sync.dma_start(wt_raw[0], rows(wt, 0))
+        load_plane(4)
+        nc.sync.dma_start(wt_raw[1], rows(wt, 1))
         nc.sync.dma_start(wx_raw[:], rows(wx, 0))
-        for s, (j0, width) in enumerate(C_PIECES):
-            nc.sync.dma_start(c_raw[s][:], rows(c, 0)[:, :, j0 : j0 + width])
-            load_plane(PACK + s)
+        load_c(0)
+        nc.sync.dma_start(bias[:], b.rearrange("(p t) -> p t", t=PACK))
+        load_plane(5)
+        load_c(1)
         load_plane(6)
         load_plane(7)
-        nc.sync.dma_start(bias[:], b.rearrange("(p t) -> p t", t=PACK))
 
-        eye_bf = sb.tile([P, KP * PACK], BF16, name="eye_bf", tag="picked0", align_bytes=64)
+        warm = sb.tile([P, 2], F32, name="warm")
+        nc.vector.memset(warm[:, 0:1], 0.0)
+        nc.scalar.activation(warm[:, 1:2], warm[:, 0:1], GELU)
+
         ident = sb.tile([P, P], BF16, name="ident")
         make_identity(nc, ident[:])
-        nc.vector.memset(eye_bf[:].bitcast(U32), 0)
-        for i in range(PACK):
-            nc.vector.tensor_copy(eye_bf[:].rearrange("p (s m i) -> p s m i", s=PACK, i=PACK)[:, i, :, i], ident[:])
         eye = mx_tiles("eye", KP)
-        quantize(eye, 0, eye_bf[:])
+        eye_bf = [staged_bf(J * i + FIRST // 2, KP // 2) for i in range(PACK)]
+        for i in range(PACK):
+            nc.vector.memset(staged(J * i + FIRST // 2, KP // 2).bitcast(U32), 0)
+        for i in range(PACK):
+            nc.vector.tensor_copy(eye_bf[i].rearrange("p (m i) -> p m i", i=PACK)[:, :, i], ident[:])
+        for i in range(PACK):
+            quantize(eye, P * i, eye_bf[i])
 
-        def deal_weights(copy, raw, name):
-            w_bf = sb.tile([P, N * PACK], BF16, name=name, align_bytes=64)
-            copy(
-                w_bf[:].rearrange("p (t m i) -> p m i t", t=PACK, i=PACK),
-                raw[:].rearrange("p i (m t) -> p m i t", t=PACK),
-            )
-            return w_bf
+        def dealt(w_bf):
+            return w_bf.rearrange("p (t m i) -> p m i t", t=PACK, i=PACK)
+
+        def by_slice(raw):
+            return raw.rearrange("p i (m t) -> p m i t", t=PACK)
 
         def weave(copy, dst, src):
             copy(
@@ -107,33 +122,39 @@ def tile_list_tier_geluP_kernel(tc, xT, wgt, wt, c, wx, b, offs, out_0, out_1, o
                 src.rearrange("p i (g r) -> p g i r", r=4),
             )
 
-        def pick(dst, n, j0, width):
+        def picked_cols(a, j0, width):
+            return picked[a][:].rearrange("p (i j) -> p i j", i=PACK)[:, :, j0 : j0 + width]
+
+        def pick(n, j0, width):
+            at = J * n + j0
             nc.vector.tensor_tensor(
-                dst,
+                staged(at, width),
                 planes[n][:].indirect(offsets[:, j0 // 16 : (j0 + width) // 16]),
-                wgt_sb[j0 // HALF][:, j0 % HALF : j0 % HALF + width],
+                wgt_sb[:, j0 : j0 + width],
                 ALU.mult,
             )
 
         xg = [mx_tiles("xg%d" % a, J) for a in range(2)]
         wq = [mx_tiles("wq%d" % a, N) for a in range(2)]
         wr = [mx_tiles("wr%d" % a, N) for a in range(2)]
-        picked0_both = sb.tile([P, PACK * J], F32, name="picked0", align_bytes=64)
-        picked0 = [picked0_both[:, PACK * HALF * h : PACK * HALF * (h + 1)].rearrange("p (i w) -> p i w", i=PACK) for h in range(2)]
 
-        def first_tier(a, copy, parts):
-            w_bf = sb.tile([P, N * PACK], BF16, name="wq_bf%d" % a, align_bytes=64)
-            per = PACK // parts
-            for u in range(parts):
-                copy(
-                    w_bf[:].rearrange("p (t m i) -> p m i t", t=PACK, i=PACK)[:, :, :, per * u : per * (u + 1)],
-                    wt_raw[a][:].rearrange("p i (m t) -> p m i t", t=PACK)[:, :, :, per * u : per * (u + 1)],
+        xg0_first = sb.tile([P, HALF * PACK], BF16, name="xg0_first", align_bytes=64)
+
+        wr_bf1 = sb.tile([P, N * PACK], BF16, name="wr_bf1", tag="plane5", align_bytes=64)
+        wr_bfs = (staged_bf(6 * J, J), wr_bf1[:])
+
+        def first_tier(a):
+            for u in range(2):
+                w_bf = ((xg0_first[:, : 2 * N], staged_bf(4 * J, N)), (staged_bf(6 * J - N // 2, N), staged_bf(6 * J + N, N)))[a][u]
+                nc.scalar.copy(
+                    w_bf.rearrange("p (t m i) -> p m i t", t=2, i=PACK),
+                    by_slice(wt_raw[a])[:, :, :, 2 * u : 2 * (u + 1)],
                 )
-                quantize(wq[a], P * per * u, w_bf[:, KP * per * u : KP * per * (u + 1)])
+                quantize(wq[a], P * 2 * u, w_bf)
 
-        def second_tier(a):
-            wr_bf = sb.tile([P, N * PACK], BF16, name="wr_bf%d" % a, tag="plane%d" % (2 + a), align_bytes=64)
-            for q in range(4):
+        def second_tier(a, banks):
+            wr_bf = wr_bfs[a]
+            for q in banks:
                 u, h = q // 2, q % 2
                 back = ps.tile([P, BANK], F32, name="back%d_%d" % (a, q), tag="bank%d" % (4 * a + q))
                 for i in range(PACK):
@@ -141,41 +162,41 @@ def tile_list_tier_geluP_kernel(tc, xT, wgt, wt, c, wx, b, offs, out_0, out_1, o
                         col = (t2 * PACK + i) * 64
                         matmul(back[:, col : col + 64], eye, P * i, wq[a], P * (2 * u + t2) + 64 * h, True, True)
                 nc.vector.tensor_tensor(
-                    wr_bf[:].rearrange("p (t m i) -> p m i t", t=PACK, i=PACK)[:, 64 * h : 64 * (h + 1), :, 2 * u : 2 * u + 2],
-                    wt_raw[a][:].rearrange("p i (m t) -> p m i t", t=PACK)[:, 64 * h : 64 * (h + 1), :, 2 * u : 2 * u + 2],
+                    dealt(wr_bf)[:, 64 * h : 64 * (h + 1), :, 2 * u : 2 * u + 2],
+                    by_slice(wt_raw[a])[:, 64 * h : 64 * (h + 1), :, 2 * u : 2 * u + 2],
                     back[:].rearrange("p (t i m) -> p m i t", t=2, i=PACK),
                     ALU.subtract,
                 )
-            return wr_bf
 
-        def pick_pass0(i):
-            for h in range(2):
-                pick(picked0[h][:, i, :], i, HALF * h, HALF)
-
-        pick_pass0(0)
-        pick_pass0(1)
-        first_tier(0, nc.vector.tensor_copy, 1)
-        pick_pass0(2)
-        wr_bf0 = second_tier(0)
-        first_tier(1, nc.scalar.copy, 2)
-        pick_pass0(3)
-        quantize(wr[0], 0, wr_bf0[:])
-        wr_bf1 = second_tier(1)
-
+        pick(0, 0, FIRST)
+        pick(0, FIRST, J - FIRST)
+        pick(1, 0, J)
+        pick(2, 0, J)
+        pick(3, 0, J)
+        first_tier(0)
+        pick(4, 0, J)
         wxq = mx_tiles("wx", N)
-        wx_bf = deal_weights(nc.scalar.copy, wx_raw, "wx_bf")
+        wx_bf = sb.tile([P, N * PACK], BF16, name="wx_bf", tag="plane3", align_bytes=64)
+        xg0_bf = (xg0_first[:], staged_bf(5 * J, J))
+        c_bf = (staged_bf(6 * J, J), staged_bf(7 * J, J))
+        cq = mx_tiles("c", J)
+        weave(nc.scalar.copy, xg0_bf[0], picked_cols(0, 0, HALF))
+        quantize(xg[0], 0, xg0_bf[0])
+        first_tier(1)
+        second_tier(0, (0, 1, 2, 3))
+        quantize(wr[0], 0, wr_bfs[0])
+        weave(nc.scalar.copy, xg0_bf[1], picked_cols(0, HALF, HALF))
+        quantize(xg[0], HALF, xg0_bf[1])
+        pick(5, 0, J)
+        nc.scalar.copy(dealt(wx_bf[:]), by_slice(wx_raw[:]))
         quantize(wxq, 0, wx_bf[:])
-        quantize(wr[1], 0, wr_bf1[:])
-        xg0_bf = sb.tile([P, J * PACK], BF16, name="xg0_bf", tag="wx_raw", align_bytes=64)
-        for h in range(2):
-            cols = slice(HALF * PACK * h, HALF * PACK * (h + 1))
-            weave(nc.scalar.copy, xg0_bf[:, cols], picked0[h])
-        quantize(xg[0], 0, xg0_bf[:])
-        c_bf = sb.tile([P, J * PACK], BF16, name="c_bf", align_bytes=64)
-        for s in range(2):
-            weave(nc.scalar.copy, c_bf[:, PACK * HALF * s : PACK * HALF * (s + 1)], c_raw[s][:])
-        cq0 = mx_tiles("c0", HALF)
-        quantize(cq0, 0, c_bf[:, : PACK * HALF])
+        second_tier(1, (0, 1, 2, 3))
+        quantize(wr[1], 0, wr_bfs[1])
+        weave(nc.scalar.copy, c_bf[0], c_raw[0][:])
+        quantize(cq, 0, c_bf[0])
+        pick(6, 0, J)
+        weave(nc.scalar.copy, c_bf[1], c_raw[1][:])
+        quantize(cq, HALF, c_bf[1])
 
         acc = []
         first_bank = 0
@@ -188,89 +209,55 @@ def tile_list_tier_geluP_kernel(tc, xT, wgt, wt, c, wx, b, offs, out_0, out_1, o
             j0, width = CHUNKS[ci]
             per_bank = BANK // width
             for n, bank in enumerate(acc[ci]):
-                for s, (lhs, rhs, first_col) in enumerate(pairs):
+                for s, (lhs, rhs) in enumerate(pairs):
                     for r in range(per_bank):
                         t = n * per_bank + r
-                        matmul(bank[:, r * width : (r + 1) * width], lhs, P * t, rhs, j0 - first_col,
+                        matmul(bank[:, r * width : (r + 1) * width], lhs, P * t, rhs, j0,
                                opens and s == 0 and r == 0, closes and s == len(pairs) - 1 and r == per_bank - 1)
 
         for ci in range(len(CHUNKS)):
-            passes(ci, [(wq[0], xg[0], 0), (wr[0], xg[0], 0)], True, False)
-        for ci in range(2):
-            passes(ci, [(wxq, cq0, 0)], False, False)
+            passes(ci, [(wq[0], xg[0]), (wr[0], xg[0])], True, False)
+        for ci in range(len(CHUNKS)):
+            passes(ci, [(wxq, cq)], False, False)
 
         yq = mx_tiles("y", J)
         out_rows = out_0.rearrange("(p t) j -> p t j", t=PACK)
         out_words = out_1[0].rearrange("p j i -> p (j i)").bitcast(I32)
 
-        def staged(tile, ci):
+        def finish_sum(ci, copy):
             j0, width = CHUNKS[ci]
-            at = PACK * (j0 - HALF) if j0 >= HALF else 0
-            return tile[:, at : at + PACK * width].rearrange("p (i w) -> p i w", i=PACK)
+            x_bf = sb.tile([P, width * PACK], BF16, name="xg1_bf%d" % ci, align_bytes=64)
+            weave(copy, x_bf[:], picked_cols(1, j0, width))
+            quantize(xg[1], j0, x_bf[:])
+            passes(ci, [(wq[1], xg[1]), (wr[1], xg[1])], False, True)
 
-        def pick_chunk(tile, ci, i):
+        def activate(ci, copy):
             j0, width = CHUNKS[ci]
-            pick(staged(tile, ci)[:, i, :], PACK + i, j0, width)
+            y = sb.tile([P, PACK, width], F32, name="y%d" % ci, align_bytes=64)
+            per_bank = BANK // width
+            for t in range(PACK):
+                r = t % per_bank
+                nc.scalar.activation(y[:, t, :], acc[ci][t // per_bank][:, r * width : (r + 1) * width], GELU, bias=bias[:, t : t + 1])
+            nc.sync.dma_start(out_rows[:, :, j0 : j0 + width], y[:])
+            y_bf = sb.tile([P, width * PACK], BF16, name="y_bf%d" % ci, align_bytes=64)
+            weave(copy, y_bf[:], y[:])
+            quantize(yq, j0, y_bf[:])
 
-        def weave_chunk(tile, ci, copy):
-            x_bf = sb.tile([P, CHUNKS[ci][1] * PACK], BF16, name="xg1_bf%d" % ci, align_bytes=64)
-            weave(copy, x_bf[:], staged(tile, ci))
-            return x_bf
-
-        def finish_sum(ci, x_bf):
-            quantize(xg[1], CHUNKS[ci][0], x_bf[:])
-            passes(ci, [(wq[1], xg[1], 0), (wr[1], xg[1], 0)], False, True)
-
-        y_bf = sb.tile([P, J * PACK], BF16, name="y_bf", align_bytes=64)
-
-        def activate(piece, chunks, copy):
-            j0 = QUARTER * piece
-            y = sb.tile([P, PACK, QUARTER], F32, name="y%d" % piece, tag=("wt_raw%d" % piece if piece < 2 else "y%d" % piece))
-            for ci in chunks:
-                at, width = CHUNKS[ci][0] - j0, CHUNKS[ci][1]
-                per_bank = BANK // width
-                for t in range(PACK):
-                    r = t % per_bank
-                    nc.scalar.activation(
-                        y[:, t, at : at + width], acc[ci][t // per_bank][:, r * width : (r + 1) * width], GELU, bias=bias[:, t : t + 1]
-                    )
-            nc.sync.dma_start(out_rows[:, :, j0 : j0 + QUARTER], y[:])
-            weave(copy, y_bf[:, PACK * j0 : PACK * (j0 + QUARTER)], y[:])
-
-        def quantize_y(j0, j1):
-            quantize(yq, j0, y_bf[:, PACK * j0 : PACK * j1])
+        on_s, on_v = nc.scalar.copy, nc.vector.tensor_copy
+        x_weave = (on_v, on_s, on_s, on_v, on_v)
+        y_weave = (on_v, on_v, on_v, on_v, on_v)
 
         def store_words(j0, j1):
             nc.sync.dma_start(out_words[:, j0:j1], yq[0][:, j0:j1].bitcast(I32))
 
-        early = [sb.tile([P, PACK * CHUNKS[ci][1]], F32, name="early%d" % ci) for ci in range(2)]
-        for i in range(PACK):
-            for ci in range(2):
-                pick_chunk(early[ci], ci, i)
-        for ci in range(2):
-            finish_sum(ci, weave_chunk(early[ci], ci, nc.scalar.copy))
-        cq1 = mx_tiles("c1", HALF, tag="wgt0")
-        quantize(cq1, 0, c_bf[:, PACK * HALF :])
-        for ci in range(2, 5):
-            passes(ci, [(wxq, cq1, HALF)], False, False)
-        late = sb.tile([P, PACK * HALF], F32, name="late", tag="early0")
-        woven = None
-        for ci in range(2, 5):
-            for i in range(PACK):
-                pick_chunk(late, ci, i)
-            if woven is not None:
-                finish_sum(ci - 1, woven)
-            woven = weave_chunk(late, ci, nc.vector.tensor_copy)
-        finish_sum(4, woven)
-        activate(0, [0], nc.scalar.copy)
-        activate(1, [1], nc.vector.tensor_copy)
-        quantize_y(0, 256)
-        activate(2, [2], nc.vector.tensor_copy)
-        quantize_y(256, 768)
-        store_words(0, 768)
-        activate(3, [3, 4], nc.scalar.copy)
-        quantize_y(768, J)
-        store_words(768, J)
+        for ci in range(len(CHUNKS)):
+            pick(7, CHUNKS[ci][0], CHUNKS[ci][1])
+            finish_sum(ci, x_weave[ci])
+        for ci in range(len(CHUNKS)):
+            activate(ci, y_weave[ci])
+            if ci == 2:
+                store_words(0, 640)
+        store_words(640, J)
         for q in range(4):
             queue = nc.sync if q % 2 == 0 else nc.scalar
             queue.dma_start(out_2[0, 4 * q : 4 * q + 4, :].bitcast(I32), yq[1][32 * q : 32 * q + 4, :].bitcast(I32))

@@ -15,6 +15,7 @@ U8 = mybir.dt.uint8
 FP8X4 = mybir.dt.float8_e4m3fn_x4
 ALU = mybir.AluOpType
 GELU = mybir.ActivationFunctionType.Gelu_apprx_tanh
+COPY = mybir.ActivationFunctionType.Copy
 
 P = 128
 PACK = 4
@@ -58,7 +59,7 @@ def tile_list_tier_geluP_kernel(tc, xT, wgt, wt, c, wx, b, offs, out_0, out_1, o
         offsets = sb.tile([P, J // 16], U16, name="offsets")
         planes = [sb.tile([P, T], F32, name="plane%d" % n, align_bytes=64) for n in range(2 * PACK)]
         wgt_sb = sb.tile([P, J], F32, name="wgt", align_bytes=64)
-        picked = [sb.tile([P, PACK * J], F32, name="picked%d" % a, tag=("picked0", "plane2")[a], align_bytes=64) for a in range(2)]
+        picked = [sb.tile([P, PACK * J], F32, name="picked%d" % a, align_bytes=64) for a in range(2)]
 
         def staged(at, words):
             return picked[at // (PACK * J)][:, at % (PACK * J) : at % (PACK * J) + words]
@@ -77,6 +78,7 @@ def tile_list_tier_geluP_kernel(tc, xT, wgt, wt, c, wx, b, offs, out_0, out_1, o
         def load_c(s):
             nc.sync.dma_start(c_raw[s][:], rows(c, 0)[:, :, HALF * s : HALF * (s + 1)])
 
+        nc.sync.dma_start(wt_raw[0], rows(wt, 0))
         nc.sync.dma_start(offsets[:], offs)
         nc.sync.dma_start(wgt_sb[:, :FIRST], wgt[:, :FIRST])
         load_plane(0)
@@ -84,22 +86,21 @@ def tile_list_tier_geluP_kernel(tc, xT, wgt, wt, c, wx, b, offs, out_0, out_1, o
         load_plane(1)
         load_plane(2)
         load_plane(3)
-        nc.sync.dma_start(wt_raw[0], rows(wt, 0))
-        load_plane(4)
         nc.sync.dma_start(wt_raw[1], rows(wt, 1))
+        load_plane(4)
         nc.sync.dma_start(wx_raw[:], rows(wx, 0))
+        load_plane(5)
         load_c(0)
         nc.sync.dma_start(bias[:], b.rearrange("(p t) -> p t", t=PACK))
-        load_plane(5)
-        load_c(1)
         load_plane(6)
+        load_c(1)
         load_plane(7)
 
         warm = sb.tile([P, 2], F32, name="warm")
         nc.vector.memset(warm[:, 0:1], 0.0)
         nc.scalar.activation(warm[:, 1:2], warm[:, 0:1], GELU)
 
-        ident = sb.tile([P, P], BF16, name="ident")
+        ident = sb.tile([P, P], F32, name="ident")
         make_identity(nc, ident[:])
         eye = mx_tiles("eye", KP)
         eye_bf = [staged_bf(J * i + FIRST // 2, KP // 2) for i in range(PACK)]
@@ -134,64 +135,108 @@ def tile_list_tier_geluP_kernel(tc, xT, wgt, wt, c, wx, b, offs, out_0, out_1, o
                 ALU.mult,
             )
 
+        def bank_tile(name, n):
+            return ps.tile([P, BANK], F32, name=name, tag="bank%d" % n)
+
         xg = [mx_tiles("xg%d" % a, J) for a in range(2)]
         wq = [mx_tiles("wq%d" % a, N) for a in range(2)]
         wr = [mx_tiles("wr%d" % a, N) for a in range(2)]
+        wr_bfs = [sb.tile([P, N * PACK], BF16, name="wr_bf%d" % a, tag=("wr_bf0", "plane4")[a], align_bytes=64)[:] for a in range(2)]
+        xg0_both = sb.tile([P, J * PACK], BF16, name="xg0_both", align_bytes=64)
+        turned = [sb.tile([P, N * PACK], BF16, name="turned", align_bytes=64)[:]]
+        minus_q = [sb.tile([P, PACK * N], F32, name="minus_q", align_bytes=64)]
+        sums = [None]
 
-        xg0_first = sb.tile([P, HALF * PACK], BF16, name="xg0_first", align_bytes=64)
+        def first_tier0():
+            w_bf = staged_bf(FIRST - 64, J)
+            nc.vector.tensor_copy(dealt(w_bf), by_slice(wt_raw[0]))
+            quantize(wq[0], 0, w_bf)
 
-        wr_bf1 = sb.tile([P, N * PACK], BF16, name="wr_bf1", tag="plane5", align_bytes=64)
-        wr_bfs = (staged_bf(6 * J, J), wr_bf1[:])
-
-        def first_tier(a):
+        def first_tier1():
             for u in range(2):
-                w_bf = ((xg0_first[:, : 2 * N], staged_bf(4 * J, N)), (staged_bf(6 * J - N // 2, N), staged_bf(6 * J + N, N)))[a][u]
+                w_bf = (xg0_both[:, 3 * N : 5 * N], staged_bf(4 * J, N))[u]
                 nc.scalar.copy(
                     w_bf.rearrange("p (t m i) -> p m i t", t=2, i=PACK),
-                    by_slice(wt_raw[a])[:, :, :, 2 * u : 2 * (u + 1)],
+                    by_slice(wt_raw[1])[:, :, :, 2 * u : 2 * (u + 1)],
                 )
-                quantize(wq[a], P * 2 * u, w_bf)
+                quantize(wq[1], P * 2 * u, w_bf)
 
-        def second_tier(a, banks):
-            wr_bf = wr_bfs[a]
-            for q in banks:
+        def second_tier1():
+            for q in range(4):
                 u, h = q // 2, q % 2
-                back = ps.tile([P, BANK], F32, name="back%d_%d" % (a, q), tag="bank%d" % (4 * a + q))
+                back = bank_tile("back1_%d" % q, 2 + q)
                 for i in range(PACK):
                     for t2 in range(2):
                         col = (t2 * PACK + i) * 64
-                        matmul(back[:, col : col + 64], eye, P * i, wq[a], P * (2 * u + t2) + 64 * h, True, True)
+                        matmul(back[:, col : col + 64], eye, P * i, wq[1], P * (2 * u + t2) + 64 * h, True, True)
                 nc.vector.tensor_tensor(
-                    dealt(wr_bf)[:, 64 * h : 64 * (h + 1), :, 2 * u : 2 * u + 2],
-                    by_slice(wt_raw[a])[:, 64 * h : 64 * (h + 1), :, 2 * u : 2 * u + 2],
+                    dealt(wr_bfs[1])[:, 64 * h : 64 * (h + 1), :, 2 * u : 2 * u + 2],
+                    by_slice(wt_raw[1])[:, 64 * h : 64 * (h + 1), :, 2 * u : 2 * u + 2],
                     back[:].rearrange("p (t i m) -> p m i t", t=2, i=PACK),
                     ALU.subtract,
                 )
 
+        def turn_weights(a):
+            sums[a] = [bank_tile("sum%d_%d" % (a, nb), PACK + nb) for nb in range(PACK)]
+            for nb in range(PACK):
+                for i in range(PACK):
+                    nc.tensor.matmul(sums[a][nb][:, P * i : P * (i + 1)], wt_raw[a][:, i, P * nb : P * (nb + 1)], ident[:],
+                                     start=(i == 0), stop=False, is_transpose=True)
+
+        def take_first_tier(a):
+            for i in range(PACK):
+                back = bank_tile("back%d_%d" % (a, i), (2 * a + i) % PACK)
+                matmul(back[:], eye, P * i, wq[a], 0, True, True)
+                nc.scalar.activation(minus_q[a][:, N * i : N * (i + 1)].rearrange("p (m t) -> p m t", t=PACK),
+                                     back[:].rearrange("p (t m) -> p m t", t=PACK), COPY, scale=-1.0)
+                for nb in range(PACK):
+                    nc.tensor.matmul(sums[a][nb][:, P * i : P * (i + 1)], minus_q[a][:, N * i + P * nb : N * i + P * (nb + 1)], ident[:],
+                                     start=False, stop=(i == PACK - 1), is_transpose=True)
+
+        def round_residual(a):
+            for nb in range(PACK):
+                nc.scalar.copy(turned[a][:, KP * nb : KP * (nb + 1)].rearrange("n (u p e) -> n u p e", u=2, e=2),
+                               sums[a][nb][:].rearrange("n (u e p) -> n u p e", u=2, e=2))
+
+        def turn_back(a):
+            for h in range(2):
+                words = bank_tile("words%d_%d" % (a, h), h)
+                for nb2 in range(2):
+                    for u in range(2):
+                        at = 2 * P * (2 * h + nb2) + P * u
+                        nc.tensor.transpose(words[:, P * (2 * nb2 + u) : P * (2 * nb2 + u + 1)], turned[a].bitcast(F32)[:, at : at + P], ident[:])
+                nc.scalar.copy(
+                    wr_bfs[a].bitcast(F32).rearrange("p (t h b m u) -> p h t b m u", t=PACK, h=2, b=2, u=2)[:, h],
+                    words[:].rearrange("p (b u m t) -> p t b m u", b=2, u=2, t=PACK),
+                )
+            quantize(wr[a], 0, wr_bfs[a])
+
+        turn_weights(0)
+        first_tier0()
+        take_first_tier(0)
         pick(0, 0, FIRST)
         pick(0, FIRST, J - FIRST)
+        round_residual(0)
         pick(1, 0, J)
         pick(2, 0, J)
         pick(3, 0, J)
-        first_tier(0)
+        turn_back(0)
+        first_tier1()
         pick(4, 0, J)
+        second_tier1()
         wxq = mx_tiles("wx", N)
-        wx_bf = sb.tile([P, N * PACK], BF16, name="wx_bf", tag="plane3", align_bytes=64)
-        xg0_bf = (xg0_first[:], staged_bf(5 * J, J))
-        c_bf = (staged_bf(6 * J, J), staged_bf(7 * J, J))
+        wx_bf = sb.tile([P, N * PACK], BF16, name="wx_bf", align_bytes=64)
+        xg0_bf = (xg0_both[:, : 2 * J], xg0_both[:, 2 * J :])
+        c_bf = [sb.tile([P, HALF * PACK], BF16, name="c_bf%d" % h, tag="plane%d" % h, align_bytes=64)[:] for h in range(2)]
         cq = mx_tiles("c", J)
+        pick(5, 0, J)
         weave(nc.scalar.copy, xg0_bf[0], picked_cols(0, 0, HALF))
         quantize(xg[0], 0, xg0_bf[0])
-        first_tier(1)
-        second_tier(0, (0, 1, 2, 3))
-        quantize(wr[0], 0, wr_bfs[0])
+        quantize(wr[1], 0, wr_bfs[1])
         weave(nc.scalar.copy, xg0_bf[1], picked_cols(0, HALF, HALF))
         quantize(xg[0], HALF, xg0_bf[1])
-        pick(5, 0, J)
         nc.scalar.copy(dealt(wx_bf[:]), by_slice(wx_raw[:]))
         quantize(wxq, 0, wx_bf[:])
-        second_tier(1, (0, 1, 2, 3))
-        quantize(wr[1], 0, wr_bfs[1])
         weave(nc.scalar.copy, c_bf[0], c_raw[0][:])
         quantize(cq, 0, c_bf[0])
         pick(6, 0, J)
@@ -233,7 +278,7 @@ def tile_list_tier_geluP_kernel(tc, xT, wgt, wt, c, wx, b, offs, out_0, out_1, o
 
         def activate(ci, copy):
             j0, width = CHUNKS[ci]
-            y = sb.tile([P, PACK, width], F32, name="y%d" % ci, align_bytes=64)
+            y = sb.tile([P, PACK, width], F32, name="y%d" % ci, tag="plane%d" % ci, align_bytes=64)
             per_bank = BANK // width
             for t in range(PACK):
                 r = t % per_bank

@@ -22,7 +22,10 @@ PACK = 4
 KP = P * PACK
 HALF = 512
 BANK = 512
-FIRST = 256
+FIRST = 512
+GROUPS = 8
+QUAD = 32
+WGT_STEP = 17
 CHUNKS = ((0, 128), (128, 256), (384, 256), (640, 256), (896, 128))
 
 
@@ -78,11 +81,14 @@ def tile_list_tier_geluP_kernel(tc, xT, wgt, wt, c, wx, b, offs, out_0, out_1, o
         def load_c(s):
             nc.sync.dma_start(c_raw[s][:], rows(c, 0)[:, :, HALF * s : HALF * (s + 1)])
 
+        wgt_rows = sb.tile([P, HALF], F32, name="wgt_rows", align_bytes=64)
+        for d in range(2):
+            nc.sync.dma_start(wgt_rows[d:QUAD:2, :], wgt.rearrange("p (h c) -> (p h) c", h=2)[::WGT_STEP, :])
+        nc.vector.memset(wgt_rows[QUAD : 2 * QUAD, :], 0.0)
+        nc.vector.memset(wgt_rows[2 * QUAD :, :], 0.0)
         nc.sync.dma_start(wt_raw[0], rows(wt, 0))
         nc.sync.dma_start(offsets[:], offs)
-        nc.sync.dma_start(wgt_sb[:, :FIRST], wgt[:, :FIRST])
         load_plane(0)
-        nc.sync.dma_start(wgt_sb[:, FIRST:], wgt[:, FIRST:])
         load_plane(1)
         load_plane(2)
         load_plane(3)
@@ -149,12 +155,13 @@ def tile_list_tier_geluP_kernel(tc, xT, wgt, wt, c, wx, b, offs, out_0, out_1, o
 
         def first_tier0():
             w_bf = staged_bf(FIRST - 64, J)
-            nc.vector.tensor_copy(dealt(w_bf), by_slice(wt_raw[0]))
+            for u in range(2):
+                nc.vector.tensor_copy(dealt(w_bf)[:, :, :, 2 * u : 2 * u + 2], by_slice(wt_raw[0])[:, :, :, 2 * u : 2 * u + 2])
             quantize(wq[0], 0, w_bf)
 
         def first_tier1():
             for u in range(2):
-                w_bf = (xg0_both[:, 3 * N : 5 * N], staged_bf(4 * J, N))[u]
+                w_bf = (xg0_both[:, 3 * N : 5 * N], wr_bfs[0][:, N : 3 * N])[u]
                 nc.scalar.copy(
                     w_bf.rearrange("p (t m i) -> p m i t", t=2, i=PACK),
                     by_slice(wt_raw[1])[:, :, :, 2 * u : 2 * (u + 1)],
@@ -184,9 +191,11 @@ def tile_list_tier_geluP_kernel(tc, xT, wgt, wt, c, wx, b, offs, out_0, out_1, o
                                      start=(i == 0), stop=False, is_transpose=True)
 
         def take_first_tier(a):
-            for i in range(PACK):
-                back = bank_tile("back%d_%d" % (a, i), (2 * a + i) % PACK)
+            backs = [bank_tile("back%d_%d" % (a, i), i) for i in range(PACK)]
+            for i, back in enumerate(backs):
                 matmul(back[:], eye, P * i, wq[a], 0, True, True)
+            turn_weights(a)
+            for i, back in enumerate(backs):
                 nc.scalar.activation(minus_q[a][:, N * i : N * (i + 1)].rearrange("p (m t) -> p m t", t=PACK),
                                      back[:].rearrange("p (t m) -> p m t", t=PACK), COPY, scale=-1.0)
                 for nb in range(PACK):
@@ -211,7 +220,22 @@ def tile_list_tier_geluP_kernel(tc, xT, wgt, wt, c, wx, b, offs, out_0, out_1, o
                 )
             quantize(wr[a], 0, wr_bfs[a])
 
-        turn_weights(0)
+        wgt_cols = sb.tile([P, J], F32, name="wgt_cols", align_bytes=64)
+        across = [bank_tile("across%d" % v, 6 + v) for v in range(2)]
+        for s in range(PACK):
+            nc.tensor.transpose(across[s // 2][:, P * (s % 2) : P * (s % 2 + 1)], wgt_rows[:, P * s : P * (s + 1)], ident[:])
+        for h in range(2):
+            for v in range(2):
+                at = HALF * h + 2 * P * v
+                nc.scalar.copy(
+                    wgt_cols[:, at : at + 2 * P].rearrange("c (s g d r) -> c s g d r", s=2, g=GROUPS, d=2),
+                    across[v][:, : 2 * P].rearrange("c (s z g h d) -> c s z g h d", s=2, g=GROUPS, h=2, d=2)[:, :, 0, :, h, :].unsqueeze(4).to_broadcast([P, 2, GROUPS, 2, GROUPS]),
+                )
+        for h in range(2):
+            spread = bank_tile("spread%d" % h, 4 + h)
+            for s in range(PACK):
+                nc.tensor.transpose(spread[:, P * s : P * (s + 1)], wgt_cols[:, HALF * h + P * s : HALF * h + P * (s + 1)], ident[:])
+            nc.scalar.copy(wgt_sb[:, HALF * h : HALF * (h + 1)], spread[:])
         first_tier0()
         take_first_tier(0)
         pick(0, 0, FIRST)
@@ -220,9 +244,9 @@ def tile_list_tier_geluP_kernel(tc, xT, wgt, wt, c, wx, b, offs, out_0, out_1, o
         pick(1, 0, J)
         pick(2, 0, J)
         pick(3, 0, J)
-        turn_back(0)
         first_tier1()
         pick(4, 0, J)
+        turn_back(0)
         second_tier1()
         wxq = mx_tiles("wx", N)
         wx_bf = sb.tile([P, N * PACK], BF16, name="wx_bf", align_bytes=64)
@@ -276,33 +300,51 @@ def tile_list_tier_geluP_kernel(tc, xT, wgt, wt, c, wx, b, offs, out_0, out_1, o
             quantize(xg[1], j0, x_bf[:])
             passes(ci, [(wq[1], xg[1]), (wr[1], xg[1])], False, True)
 
-        def activate(ci, copy):
-            j0, width = CHUNKS[ci]
-            y = sb.tile([P, PACK, width], F32, name="y%d" % ci, tag="plane%d" % ci, align_bytes=64)
-            per_bank = BANK // width
-            for t in range(PACK):
-                r = t % per_bank
-                nc.scalar.activation(y[:, t, :], acc[ci][t // per_bank][:, r * width : (r + 1) * width], GELU, bias=bias[:, t : t + 1])
-            nc.sync.dma_start(out_rows[:, :, j0 : j0 + width], y[:])
-            y_bf = sb.tile([P, width * PACK], BF16, name="y_bf%d" % ci, align_bytes=64)
-            weave(copy, y_bf[:], y[:])
-            quantize(yq, j0, y_bf[:])
+        y_bf = sb.tile([P, J * PACK], BF16, name="y_bf", align_bytes=64)
 
-        on_s, on_v = nc.scalar.copy, nc.vector.tensor_copy
-        x_weave = (on_v, on_s, on_s, on_v, on_v)
-        y_weave = (on_v, on_v, on_v, on_v, on_v)
+        def activate(chunks, copy, slot):
+            j0 = CHUNKS[chunks[0]][0]
+            span = sum(CHUNKS[ci][1] for ci in chunks)
+            y = sb.tile([P, PACK, span], F32, name="y%d" % chunks[0], tag=slot, align_bytes=64)
+            for ci in chunks:
+                at, width = CHUNKS[ci][0] - j0, CHUNKS[ci][1]
+                per_bank = BANK // width
+                for t in range(PACK):
+                    r = t % per_bank
+                    nc.scalar.activation(y[:, t, at : at + width], acc[ci][t // per_bank][:, r * width : (r + 1) * width], GELU, bias=bias[:, t : t + 1])
+            nc.sync.dma_start(out_rows[:, :, j0 : j0 + span], y[:])
+            weave(copy, y_bf[:, PACK * j0 : PACK * (j0 + span)], y[:])
+
+        def quantize_y(j0, j1):
+            quantize(yq, j0, y_bf[:, PACK * j0 : PACK * j1])
 
         def store_words(j0, j1):
             nc.sync.dma_start(out_words[:, j0:j1], yq[0][:, j0:j1].bitcast(I32))
 
-        for ci in range(len(CHUNKS)):
-            pick(7, CHUNKS[ci][0], CHUNKS[ci][1])
-            finish_sum(ci, x_weave[ci])
-        for ci in range(len(CHUNKS)):
-            activate(ci, y_weave[ci])
-            if ci == 2:
-                store_words(0, 640)
-        store_words(640, J)
+        on_s, on_v = nc.scalar.copy, nc.vector.tensor_copy
+        pick(7, 0, 128)
+        finish_sum(0, on_v)
+        pick(7, 128, 256)
+        finish_sum(1, on_s)
+        pick(7, 384, 256)
+        finish_sum(2, on_s)
+        pick(7, 640, 256)
+        finish_sum(3, on_v)
+        pick(7, 896, 128)
+        finish_sum(4, on_v)
+        activate([0], on_v, "plane0")
+        quantize_y(0, 128)
+        activate([1], on_v, "plane1")
+        quantize_y(128, 384)
+        activate([2], on_v, "plane2")
+        quantize_y(384, 640)
+        store_words(0, 640)
+        activate([3], on_v, "plane3")
+        quantize_y(640, 896)
+        store_words(640, 896)
+        activate([4], on_v, "y4")
+        quantize_y(896, 1024)
+        store_words(896, 1024)
         for q in range(4):
             queue = nc.sync if q % 2 == 0 else nc.scalar
             queue.dma_start(out_2[0, 4 * q : 4 * q + 4, :].bitcast(I32), yq[1][32 * q : 32 * q + 4, :].bitcast(I32))

@@ -23,6 +23,7 @@ KP = P * PACK
 HALF = 512
 BANK = 512
 FIRST = 512
+C_PIECES = ((0, 640), (640, 384))
 GROUPS = 8
 QUAD = 32
 WGT_STEP = 17
@@ -72,14 +73,14 @@ def tile_list_tier_geluP_kernel(tc, xT, wgt, wt, c, wx, b, offs, out_0, out_1, o
 
         wt_raw = [sb.tile([P, PACK, N], F32, name="wt_raw%d" % a, align_bytes=64)[:] for a in range(2)]
         wx_raw = sb.tile([P, PACK, N], F32, name="wx_raw", align_bytes=64)
-        c_raw = [sb.tile([P, PACK, HALF], F32, name="c_raw%d" % s) for s in range(2)]
+        c_raw = [sb.tile([P, PACK, width], F32, name="c_raw%d" % s) for s, (j0, width) in enumerate(C_PIECES)]
         bias = sb.tile([P, PACK], F32, name="bias")
 
         def load_plane(n):
             nc.sync.dma_start(planes[n][:], rows(xT, n // PACK)[:, n % PACK, :])
 
         def load_c(s):
-            nc.sync.dma_start(c_raw[s][:], rows(c, 0)[:, :, HALF * s : HALF * (s + 1)])
+            nc.sync.dma_start(c_raw[s][:], rows(c, 0)[:, :, C_PIECES[s][0] : C_PIECES[s][0] + C_PIECES[s][1]])
 
         wgt_rows = sb.tile([P, HALF], F32, name="wgt_rows", align_bytes=64)
         for d in range(2):
@@ -99,8 +100,8 @@ def tile_list_tier_geluP_kernel(tc, xT, wgt, wt, c, wx, b, offs, out_0, out_1, o
         load_c(0)
         nc.sync.dma_start(bias[:], b.rearrange("(p t) -> p t", t=PACK))
         load_plane(6)
-        load_c(1)
         load_plane(7)
+        load_c(1)
 
         warm = sb.tile([P, 2], F32, name="warm")
         nc.vector.memset(warm[:, 0:1], 0.0)
@@ -251,7 +252,7 @@ def tile_list_tier_geluP_kernel(tc, xT, wgt, wt, c, wx, b, offs, out_0, out_1, o
         wxq = mx_tiles("wx", N)
         wx_bf = sb.tile([P, N * PACK], BF16, name="wx_bf", align_bytes=64)
         xg0_bf = (xg0_both[:, : 2 * J], xg0_both[:, 2 * J :])
-        c_bf = [sb.tile([P, HALF * PACK], BF16, name="c_bf%d" % h, tag="plane%d" % h, align_bytes=64)[:] for h in range(2)]
+        c_bf = [sb.tile([P, C_PIECES[h][1] * PACK], BF16, name="c_bf%d" % h, tag="plane%d" % h, align_bytes=64)[:] for h in range(2)]
         cq = mx_tiles("c", J)
         pick(5, 0, J)
         weave(nc.scalar.copy, xg0_bf[0], picked_cols(0, 0, HALF))
@@ -262,10 +263,9 @@ def tile_list_tier_geluP_kernel(tc, xT, wgt, wt, c, wx, b, offs, out_0, out_1, o
         nc.scalar.copy(dealt(wx_bf[:]), by_slice(wx_raw[:]))
         quantize(wxq, 0, wx_bf[:])
         weave(nc.scalar.copy, c_bf[0], c_raw[0][:])
-        quantize(cq, 0, c_bf[0])
+        quantize(cq, 0, c_bf[0][:, : PACK * HALF])
+        quantize(cq, HALF, c_bf[0][:, PACK * HALF :])
         pick(6, 0, J)
-        weave(nc.scalar.copy, c_bf[1], c_raw[1][:])
-        quantize(cq, HALF, c_bf[1])
 
         acc = []
         first_bank = 0
@@ -286,7 +286,7 @@ def tile_list_tier_geluP_kernel(tc, xT, wgt, wt, c, wx, b, offs, out_0, out_1, o
 
         for ci in range(len(CHUNKS)):
             passes(ci, [(wq[0], xg[0]), (wr[0], xg[0])], True, False)
-        for ci in range(len(CHUNKS)):
+        for ci in range(3):
             passes(ci, [(wxq, cq)], False, False)
 
         yq = mx_tiles("y", J)
@@ -329,12 +329,17 @@ def tile_list_tier_geluP_kernel(tc, xT, wgt, wt, c, wx, b, offs, out_0, out_1, o
         pick(7, 384, 256)
         finish_sum(2, on_s)
         pick(7, 640, 256)
-        finish_sum(3, on_v)
         pick(7, 896, 128)
+        weave(on_v, c_bf[1], c_raw[1][:])
+        quantize(cq, 640, c_bf[1][:, : PACK * 256])
+        quantize(cq, 896, c_bf[1][:, PACK * 256 :])
+        passes(3, [(wxq, cq)], False, False)
+        passes(4, [(wxq, cq)], False, False)
+        finish_sum(3, on_v)
         finish_sum(4, on_v)
         activate([0], on_v, "plane0")
         quantize_y(0, 128)
-        activate([1], on_v, "plane1")
+        activate([1], on_v, "plane5")
         quantize_y(128, 384)
         activate([2], on_v, "plane2")
         quantize_y(384, 640)

@@ -73,7 +73,7 @@ def tile_list_tier_geluP_kernel(tc, xT, wgt, wt, c, wx, b, offs, out_0, out_1, o
 
         wt_raw = [sb.tile([P, PACK, N], F32, name="wt_raw%d" % a, align_bytes=64)[:] for a in range(2)]
         wx_raw = sb.tile([P, PACK, N], F32, name="wx_raw", align_bytes=64)
-        c_raw = [sb.tile([P, PACK, width], F32, name="c_raw%d" % s) for s, (j0, width) in enumerate(C_PIECES)]
+        c_raw = [sb.tile([P, PACK, width], F32, name="c_raw%d" % s, align_bytes=64) for s, (j0, width) in enumerate(C_PIECES)]
         bias = sb.tile([P, PACK], F32, name="bias")
 
         def load_plane(n):
@@ -84,7 +84,7 @@ def tile_list_tier_geluP_kernel(tc, xT, wgt, wt, c, wx, b, offs, out_0, out_1, o
 
         wgt_rows = sb.tile([P, HALF], F32, name="wgt_rows", align_bytes=64)
         for d in range(2):
-            nc.sync.dma_start(wgt_rows[d:QUAD:2, :], wgt.rearrange("p (h c) -> (p h) c", h=2)[::WGT_STEP, :])
+            nc.scalar.dma_start(wgt_rows[d:QUAD:2, :], wgt.rearrange("p (h c) -> (p h) c", h=2)[::WGT_STEP, :])
         nc.vector.memset(wgt_rows[QUAD : 2 * QUAD, :], 0.0)
         nc.vector.memset(wgt_rows[2 * QUAD :, :], 0.0)
         nc.sync.dma_start(wt_raw[0], rows(wt, 0))
@@ -98,10 +98,10 @@ def tile_list_tier_geluP_kernel(tc, xT, wgt, wt, c, wx, b, offs, out_0, out_1, o
         nc.sync.dma_start(wx_raw[:], rows(wx, 0))
         load_plane(5)
         load_c(0)
-        nc.sync.dma_start(bias[:], b.rearrange("(p t) -> p t", t=PACK))
         load_plane(6)
         load_plane(7)
         load_c(1)
+        nc.sync.dma_start(bias[:], b.rearrange("(p t) -> p t", t=PACK))
 
         warm = sb.tile([P, 2], F32, name="warm")
         nc.vector.memset(warm[:, 0:1], 0.0)
@@ -265,6 +265,15 @@ def tile_list_tier_geluP_kernel(tc, xT, wgt, wt, c, wx, b, offs, out_0, out_1, o
         weave(nc.scalar.copy, c_bf[0], c_raw[0][:])
         quantize(cq, 0, c_bf[0][:, : PACK * HALF])
         quantize(cq, HALF, c_bf[0][:, PACK * HALF :])
+        xg1_bf = sb.tile([P, J * PACK], BF16, name="xg1_bf", tag="c_raw0", align_bytes=64)
+
+        def weave_pair(copy, pair, j0, width):
+            copy(
+                xg1_bf[:, PACK * j0 : PACK * (j0 + width)].rearrange("p (j i) -> p j i", i=PACK)[:, :, 2 * pair : 2 * pair + 2],
+                picked_cols(1, j0, width)[:, 2 * pair : 2 * pair + 2, :].rearrange("p i j -> p j i"),
+            )
+
+        weave_pair(nc.scalar.copy, 0, 0, J)
         pick(6, 0, J)
 
         acc = []
@@ -295,9 +304,8 @@ def tile_list_tier_geluP_kernel(tc, xT, wgt, wt, c, wx, b, offs, out_0, out_1, o
 
         def finish_sum(ci, copy):
             j0, width = CHUNKS[ci]
-            x_bf = sb.tile([P, width * PACK], BF16, name="xg1_bf%d" % ci, align_bytes=64)
-            weave(copy, x_bf[:], picked_cols(1, j0, width))
-            quantize(xg[1], j0, x_bf[:])
+            weave_pair(copy, 1, j0, width)
+            quantize(xg[1], j0, xg1_bf[:, PACK * j0 : PACK * (j0 + width)])
             passes(ci, [(wq[1], xg[1]), (wr[1], xg[1])], False, True)
 
         y_bf = sb.tile([P, J * PACK], BF16, name="y_bf", align_bytes=64)
@@ -337,16 +345,14 @@ def tile_list_tier_geluP_kernel(tc, xT, wgt, wt, c, wx, b, offs, out_0, out_1, o
         passes(4, [(wxq, cq)], False, False)
         finish_sum(3, on_v)
         finish_sum(4, on_v)
-        activate([0], on_v, "plane0")
-        quantize_y(0, 128)
+        activate([0], on_s, "plane0")
         activate([1], on_v, "plane5")
-        quantize_y(128, 384)
         activate([2], on_v, "plane2")
-        quantize_y(384, 640)
-        store_words(0, 640)
+        quantize_y(0, 512)
+        quantize_y(512, 640)
         activate([3], on_v, "plane3")
         quantize_y(640, 896)
-        store_words(640, 896)
+        store_words(0, 896)
         activate([4], on_v, "y4")
         quantize_y(896, 1024)
         store_words(896, 1024)

@@ -196,15 +196,17 @@ def tile_list_tier_geluP_kernel(tc, xT, wgt, wt, c, wx, b, offs, out_0, out_1, o
             for i, back in enumerate(backs):
                 matmul(back[:], eye, P * i, wq[a], 0, True, True)
             turn_weights(a)
-            for i, back in enumerate(backs):
-                nc.scalar.activation(minus_q[a][:, N * i : N * (i + 1)].rearrange("p (m t) -> p m t", t=PACK),
-                                     back[:].rearrange("p (t m) -> p m t", t=PACK), COPY, scale=-1.0)
-                for nb in range(PACK):
-                    nc.tensor.matmul(sums[a][nb][:, P * i : P * (i + 1)], minus_q[a][:, N * i + P * nb : N * i + P * (nb + 1)], ident[:],
-                                     start=False, stop=(i == PACK - 1), is_transpose=True)
+            for h in (1, 0):
+                for i, back in enumerate(backs):
+                    at = N * i + 2 * P * h
+                    nc.scalar.activation(minus_q[a][:, at : at + 2 * P].rearrange("p (m t) -> p m t", t=PACK),
+                                         back[:].rearrange("p (t m) -> p m t", t=PACK)[:, 64 * h : 64 * (h + 1), :], COPY, scale=-1.0)
+                    for nb in range(2 * h, 2 * h + 2):
+                        nc.tensor.matmul(sums[a][nb][:, P * i : P * (i + 1)], minus_q[a][:, N * i + P * nb : N * i + P * (nb + 1)], ident[:],
+                                         start=False, stop=(i == PACK - 1), is_transpose=True)
 
         def round_residual(a):
-            for nb in range(PACK):
+            for nb in (2, 3, 0, 1):
                 nc.scalar.copy(turned[a][:, KP * nb : KP * (nb + 1)].rearrange("n (u p e) -> n u p e", u=2, e=2),
                                sums[a][nb][:].rearrange("n (u e p) -> n u p e", u=2, e=2))
 

@@ -312,6 +312,8 @@ def tile_list_tier_geluP_kernel(tc, xT, wgt, wt, c, wx, b, offs, out_0, out_1, o
 
         y_bf = sb.tile([P, J * PACK], BF16, name="y_bf", align_bytes=64)
 
+        ys = {}
+
         def activate(chunks, copy, slot):
             j0 = CHUNKS[chunks[0]][0]
             span = sum(CHUNKS[ci][1] for ci in chunks)
@@ -323,7 +325,13 @@ def tile_list_tier_geluP_kernel(tc, xT, wgt, wt, c, wx, b, offs, out_0, out_1, o
                     r = t % per_bank
                     nc.scalar.activation(y[:, t, at : at + width], acc[ci][t // per_bank][:, r * width : (r + 1) * width], GELU, bias=bias[:, t : t + 1])
             nc.sync.dma_start(out_rows[:, :, j0 : j0 + span], y[:])
-            weave(copy, y_bf[:, PACK * j0 : PACK * (j0 + span)], y[:])
+            ys[chunks[0]] = y
+            if copy is not None:
+                weave_y(chunks[0], copy)
+
+        def weave_y(ci, copy):
+            j0, width = CHUNKS[ci]
+            weave(copy, y_bf[:, PACK * j0 : PACK * (j0 + width)], ys[ci][:])
 
         def quantize_y(j0, j1):
             quantize(yq, j0, y_bf[:, PACK * j0 : PACK * j1])
@@ -347,17 +355,20 @@ def tile_list_tier_geluP_kernel(tc, xT, wgt, wt, c, wx, b, offs, out_0, out_1, o
         passes(4, [(wxq, cq)], False, False)
         finish_sum(3, on_v)
         finish_sum(4, on_v)
-        activate([0], on_s, "plane0")
+        activate([0], None, "plane0")
         activate([1], on_v, "plane5")
+        quantize_y(128, 384)
         activate([2], on_v, "plane2")
-        quantize_y(0, 512)
-        quantize_y(512, 640)
+        quantize_y(384, 640)
         activate([3], on_v, "plane3")
         quantize_y(640, 896)
-        store_words(0, 896)
+        store_words(128, 896)
         activate([4], on_v, "y4")
         quantize_y(896, 1024)
         store_words(896, 1024)
+        weave_y(0, on_s)
+        quantize_y(0, 128)
+        store_words(0, 128)
         for q in range(4):
             queue = nc.sync if q % 2 == 0 else nc.scalar
             queue.dma_start(out_2[0, 4 * q : 4 * q + 4, :].bitcast(I32), yq[1][32 * q : 32 * q + 4, :].bitcast(I32))

@@ -324,7 +324,8 @@ def tile_list_tier_geluP_kernel(tc, xT, wgt, wt, c, wx, b, offs, out_0, out_1, o
                 for t in range(PACK):
                     r = t % per_bank
                     nc.scalar.activation(y[:, t, at : at + width], acc[ci][t // per_bank][:, r * width : (r + 1) * width], GELU, bias=bias[:, t : t + 1])
-            nc.sync.dma_start(out_rows[:, :, j0 : j0 + span], y[:])
+                    if t % 2 == 1:
+                        nc.sync.dma_start(out_rows[:, t - 1 : t + 1, j0 : j0 + span], y[:, t - 1 : t + 1, :])
             ys[chunks[0]] = y
             if copy is not None:
                 weave_y(chunks[0], copy)

@@ -23,11 +23,11 @@ KP = P * PACK
 HALF = 512
 BANK = 512
 FIRST = 512
-C_PIECES = ((0, 640), (640, 384))
+C_PIECES = ((256, 512), (0, 128), (768, 256), (128, 128))
 GROUPS = 8
 QUAD = 32
 WGT_STEP = 17
-CHUNKS = ((0, 128), (128, 256), (384, 256), (640, 256), (896, 128))
+CHUNKS = ((0, 128), (256, 256), (512, 256), (768, 256), (128, 128))
 
 
 def tile_list_tier_geluP_kernel(tc, xT, wgt, wt, c, wx, b, offs, out_0, out_1, out_2):
@@ -73,14 +73,16 @@ def tile_list_tier_geluP_kernel(tc, xT, wgt, wt, c, wx, b, offs, out_0, out_1, o
 
         wt_raw = [sb.tile([P, PACK, N], F32, name="wt_raw%d" % a, align_bytes=64)[:] for a in range(2)]
         wx_raw = sb.tile([P, PACK, N], F32, name="wx_raw", align_bytes=64)
-        c_raw = [sb.tile([P, PACK, width], F32, name="c_raw%d" % s, align_bytes=64) for s, (j0, width) in enumerate(C_PIECES)]
+        c_raw = [sb.tile([P, PACK, width], F32, name="c_raw%d" % h, align_bytes=64) for h, width in enumerate((640, 384))]
         bias = sb.tile([P, PACK], F32, name="bias")
 
         def load_plane(n):
             nc.sync.dma_start(planes[n][:], rows(xT, n // PACK)[:, n % PACK, :])
 
         def load_c(s):
-            nc.sync.dma_start(c_raw[s][:], rows(c, 0)[:, :, C_PIECES[s][0] : C_PIECES[s][0] + C_PIECES[s][1]])
+            j0, width = C_PIECES[s]
+            at = C_PIECES[s - 1][1] * (s % 2)
+            nc.sync.dma_start(c_raw[s // 2][:, :, at : at + width], rows(c, 0)[:, :, j0 : j0 + width])
 
         wgt_rows = sb.tile([P, HALF], F32, name="wgt_rows", align_bytes=64)
         for d in range(2):
@@ -97,10 +99,12 @@ def tile_list_tier_geluP_kernel(tc, xT, wgt, wt, c, wx, b, offs, out_0, out_1, o
         load_plane(4)
         nc.sync.dma_start(wx_raw[:], rows(wx, 0))
         load_plane(5)
+        load_c(1)
         load_c(0)
         load_plane(6)
         load_plane(7)
-        load_c(1)
+        load_c(2)
+        load_c(3)
         nc.sync.dma_start(bias[:], b.rearrange("(p t) -> p t", t=PACK))
 
         warm = sb.tile([P, 2], F32, name="warm")
@@ -254,7 +258,8 @@ def tile_list_tier_geluP_kernel(tc, xT, wgt, wt, c, wx, b, offs, out_0, out_1, o
         wxq = mx_tiles("wx", N)
         wx_bf = sb.tile([P, N * PACK], BF16, name="wx_bf", align_bytes=64)
         xg0_bf = (xg0_both[:, : 2 * J], xg0_both[:, 2 * J :])
-        c_bf = [sb.tile([P, C_PIECES[h][1] * PACK], BF16, name="c_bf%d" % h, tag="plane%d" % h, align_bytes=64)[:] for h in range(2)]
+        c_both = [sb.tile([P, 640 * PACK], BF16, name="c_bf%d" % h, tag="plane%d" % h, align_bytes=64) for h in range(2)]
+        c_bf = [c_both[0][:, : PACK * 512], c_both[0][:, PACK * 512 :], c_both[1][:, : PACK * 256], c_both[1][:, PACK * 256 : PACK * 384]]
         cq = mx_tiles("c", J)
         pick(5, 0, J)
         weave(nc.scalar.copy, xg0_bf[0], picked_cols(0, 0, HALF))
@@ -264,9 +269,9 @@ def tile_list_tier_geluP_kernel(tc, xT, wgt, wt, c, wx, b, offs, out_0, out_1, o
         quantize(xg[0], HALF, xg0_bf[1])
         nc.scalar.copy(dealt(wx_bf[:]), by_slice(wx_raw[:]))
         quantize(wxq, 0, wx_bf[:])
-        weave(nc.scalar.copy, c_bf[0], c_raw[0][:])
-        quantize(cq, 0, c_bf[0][:, : PACK * HALF])
-        quantize(cq, HALF, c_bf[0][:, PACK * HALF :])
+        weave(nc.scalar.copy, c_both[0][:], c_raw[0][:])
+        for s in range(2):
+            quantize(cq, C_PIECES[s][0], c_bf[s])
         xg1_bf = sb.tile([P, J * PACK], BF16, name="xg1_bf", tag="c_raw0", align_bytes=64)
 
         def weave_pair(copy, pair, j0, width):
@@ -324,8 +329,8 @@ def tile_list_tier_geluP_kernel(tc, xT, wgt, wt, c, wx, b, offs, out_0, out_1, o
                 for t in range(PACK):
                     r = t % per_bank
                     nc.scalar.activation(y[:, t, at : at + width], acc[ci][t // per_bank][:, r * width : (r + 1) * width], GELU, bias=bias[:, t : t + 1])
-                    if t % 2 == 1:
-                        nc.sync.dma_start(out_rows[:, t - 1 : t + 1, j0 : j0 + span], y[:, t - 1 : t + 1, :])
+                    if r == per_bank - 1:
+                        nc.sync.dma_start(out_rows[:, t - r : t + 1, j0 : j0 + span], y[:, t - r : t + 1, :])
             ys[chunks[0]] = y
             if copy is not None:
                 weave_y(chunks[0], copy)
@@ -341,35 +346,32 @@ def tile_list_tier_geluP_kernel(tc, xT, wgt, wt, c, wx, b, offs, out_0, out_1, o
             nc.sync.dma_start(out_words[:, j0:j1], yq[0][:, j0:j1].bitcast(I32))
 
         on_s, on_v = nc.scalar.copy, nc.vector.tensor_copy
-        pick(7, 0, 128)
+        pick(7, *CHUNKS[0])
         finish_sum(0, on_v)
-        pick(7, 128, 256)
+        pick(7, *CHUNKS[1])
         finish_sum(1, on_s)
-        pick(7, 384, 256)
+        pick(7, *CHUNKS[2])
         finish_sum(2, on_s)
-        pick(7, 640, 256)
-        pick(7, 896, 128)
-        weave(on_v, c_bf[1], c_raw[1][:])
-        quantize(cq, 640, c_bf[1][:, : PACK * 256])
-        quantize(cq, 896, c_bf[1][:, PACK * 256 :])
+        pick(7, *CHUNKS[3])
+        pick(7, *CHUNKS[4])
+        weave(on_v, c_both[1][:, : PACK * 384], c_raw[1][:])
+        for s in (2, 3):
+            quantize(cq, C_PIECES[s][0], c_bf[s])
         passes(3, [(wxq, cq)], False, False)
         passes(4, [(wxq, cq)], False, False)
         finish_sum(3, on_v)
         finish_sum(4, on_v)
         activate([0], None, "plane0")
         activate([1], on_v, "plane5")
-        quantize_y(128, 384)
         activate([2], on_v, "plane2")
-        quantize_y(384, 640)
+        quantize_y(256, 768)
         activate([3], on_v, "plane3")
-        quantize_y(640, 896)
-        store_words(128, 896)
+        quantize_y(768, 1024)
+        store_words(256, 1024)
         activate([4], on_v, "y4")
-        quantize_y(896, 1024)
-        store_words(896, 1024)
         weave_y(0, on_s)
-        quantize_y(0, 128)
-        store_words(0, 128)
+        quantize_y(0, 256)
+        store_words(0, 256)
         for q in range(4):
             queue = nc.sync if q % 2 == 0 else nc.scalar
             queue.dma_start(out_2[0, 4 * q : 4 * q + 4, :].bitcast(I32), yq[1][32 * q : 32 * q + 4, :].bitcast(I32))

@@ -368,9 +368,11 @@ def tile_list_tier_geluP_kernel(tc, xT, wgt, wt, c, wx, b, offs, out_0, out_1, o
         activate([3], on_v, "plane3")
         quantize_y(768, 1024)
         store_words(256, 1024)
-        activate([4], on_v, "y4")
+        activate([4], None, "y4")
         weave_y(0, on_s)
-        quantize_y(0, 256)
+        quantize_y(0, 128)
+        weave_y(4, on_v)
+        quantize_y(128, 256)
         store_words(0, 256)
         for q in range(4):
             queue = nc.sync if q % 2 == 0 else nc.scalar

@@ -23,11 +23,11 @@ KP = P * PACK
 HALF = 512
 BANK = 512
 FIRST = 512
-C_PIECES = ((256, 512), (0, 128), (768, 256), (128, 128))
+C_PIECES = ((512, 512), (0, 128), (128, 384))
 GROUPS = 8
 QUAD = 32
 WGT_STEP = 17
-CHUNKS = ((0, 128), (256, 256), (512, 256), (768, 256), (128, 128))
+CHUNKS = ((0, 128), (512, 256), (768, 256), (256, 256), (128, 128))
 
 
 def tile_list_tier_geluP_kernel(tc, xT, wgt, wt, c, wx, b, offs, out_0, out_1, out_2):
@@ -104,7 +104,6 @@ def tile_list_tier_geluP_kernel(tc, xT, wgt, wt, c, wx, b, offs, out_0, out_1, o
         load_plane(6)
         load_plane(7)
         load_c(2)
-        load_c(3)
         nc.sync.dma_start(bias[:], b.rearrange("(p t) -> p t", t=PACK))
 
         warm = sb.tile([P, 2], F32, name="warm")
@@ -259,7 +258,7 @@ def tile_list_tier_geluP_kernel(tc, xT, wgt, wt, c, wx, b, offs, out_0, out_1, o
         wx_bf = sb.tile([P, N * PACK], BF16, name="wx_bf", align_bytes=64)
         xg0_bf = (xg0_both[:, : 2 * J], xg0_both[:, 2 * J :])
         c_both = [sb.tile([P, 640 * PACK], BF16, name="c_bf%d" % h, tag="plane%d" % h, align_bytes=64) for h in range(2)]
-        c_bf = [c_both[0][:, : PACK * 512], c_both[0][:, PACK * 512 :], c_both[1][:, : PACK * 256], c_both[1][:, PACK * 256 : PACK * 384]]
+        c_bf = [c_both[0][:, : PACK * 512], c_both[0][:, PACK * 512 :], c_both[1][:, PACK * 128 : PACK * 384], c_both[1][:, : PACK * 128]]
         cq = mx_tiles("c", J)
         pick(5, 0, J)
         weave(nc.scalar.copy, xg0_bf[0], picked_cols(0, 0, HALF))
@@ -352,11 +351,10 @@ def tile_list_tier_geluP_kernel(tc, xT, wgt, wt, c, wx, b, offs, out_0, out_1, o
         finish_sum(1, on_s)
         pick(7, *CHUNKS[2])
         finish_sum(2, on_s)
-        pick(7, *CHUNKS[3])
-        pick(7, *CHUNKS[4])
+        pick(7, *C_PIECES[2])
         weave(on_v, c_both[1][:, : PACK * 384], c_raw[1][:])
         for s in (2, 3):
-            quantize(cq, C_PIECES[s][0], c_bf[s])
+            quantize(cq, CHUNKS[s + 1][0], c_bf[s])
         passes(3, [(wxq, cq)], False, False)
         passes(4, [(wxq, cq)], False, False)
         finish_sum(3, on_v)
@@ -364,16 +362,16 @@ def tile_list_tier_geluP_kernel(tc, xT, wgt, wt, c, wx, b, offs, out_0, out_1, o
         activate([0], None, "plane0")
         activate([1], on_v, "plane5")
         activate([2], on_v, "plane2")
-        quantize_y(256, 768)
+        quantize_y(512, 1024)
         activate([3], on_v, "plane3")
-        quantize_y(768, 1024)
-        store_words(256, 1024)
+        store_words(512, 1024)
+        quantize_y(256, 512)
         activate([4], None, "y4")
         weave_y(0, on_s)
         quantize_y(0, 128)
         weave_y(4, on_v)
         quantize_y(128, 256)
-        store_words(0, 256)
+        store_words(0, 512)
         for q in range(4):
             queue = nc.sync if q % 2 == 0 else nc.scalar
             queue.dma_start(out_2[0, 4 * q : 4 * q + 4, :].bitcast(I32), yq[1][32 * q : 32 * q + 4, :].bitcast(I32))

@@ -22,24 +22,27 @@ PACK = 4
 KP = P * PACK
 HALF = 512
 BANK = 512
-FIRST = 512
-C_PIECES = ((512, 512), (0, 128), (128, 384))
 GROUPS = 8
 QUAD = 32
 WGT_STEP = 17
+KIB = 1024
 CHUNKS = ((0, 128), (512, 256), (768, 256), (256, 256), (128, 128))
+EARLY = ((0, 128), (512, 512))
+LATE = (128, 384)
 
 
 def tile_list_tier_geluP_kernel(tc, xT, wgt, wt, c, wx, b, offs, out_0, out_1, out_2):
     nc = tc.nc
     with ExitStack() as ctx:
+        held = ctx.enter_context(tc.tile_pool(name="held", bufs=1))
         sb = ctx.enter_context(tc.tile_pool(name="sb", bufs=1))
         ps = ctx.enter_context(tc.psum_pool(name="ps", bufs=1))
 
-        def mx_tiles(name, width):
-            codes = sb.tile([P, width], U32, name=name + "_codes", align_bytes=64)
-            scales = sb.tile([P, width], U8, name=name + "_scales", align_bytes=64)
-            return codes, scales
+        def place(name, shape, dtype, kib):
+            return sb.tile(shape, dtype, name=name, align_bytes=64, offset=int(kib * KIB))
+
+        def mx_tiles(name, width, kib):
+            return place(name + "_codes", [P, width], U32, kib), place(name + "_scales", [P, width], U8, kib + width * 4 / KIB)
 
         def quantize(dst, col, src):
             width = src.shape[1] // PACK
@@ -60,66 +63,56 @@ def tile_list_tier_geluP_kernel(tc, xT, wgt, wt, c, wx, b, offs, out_0, out_1, o
         def rows(src, a):
             return src[KP * a : KP * (a + 1), :].rearrange("(p i) w -> p i w", i=PACK)
 
-        offsets = sb.tile([P, J // 16], U16, name="offsets")
-        planes = [sb.tile([P, T], F32, name="plane%d" % n, align_bytes=64) for n in range(2 * PACK)]
-        wgt_sb = sb.tile([P, J], F32, name="wgt", align_bytes=64)
-        picked = [sb.tile([P, PACK * J], F32, name="picked%d" % a, align_bytes=64) for a in range(2)]
+        def bank_tile(name, n):
+            return ps.tile([P, BANK], F32, name=name, tag="bank%d" % n)
 
-        def staged(at, words):
-            return picked[at // (PACK * J)][:, at % (PACK * J) : at % (PACK * J) + words]
-
-        def staged_bf(at, words):
-            return staged(at, words).bitcast(BF16)
-
-        wt_raw = [sb.tile([P, PACK, N], F32, name="wt_raw%d" % a, align_bytes=64)[:] for a in range(2)]
-        wx_raw = sb.tile([P, PACK, N], F32, name="wx_raw", align_bytes=64)
-        c_raw = [sb.tile([P, PACK, width], F32, name="c_raw%d" % h, align_bytes=64) for h, width in enumerate((640, 384))]
-        bias = sb.tile([P, PACK], F32, name="bias")
+        offsets = held.tile([P, J // 16], U16, name="offsets")
+        planes = [place("plane%d" % n, [P, T], F32, 8 * n) for n in range(2 * PACK)]
+        wt_raw = [place("wt_raw0", [P, PACK, N], F32, 216)]
+        wt_halves = [place("wt_half%d" % h, [P, PACK, 2 * P], F32, 104 + 4 * h) for h in range(2)]
+        wx_raw = place("wx_raw", [P, PACK, N], F32, 112)
+        c_early = place("c_early", [P, PACK, 640], F32, 120)
+        c_late = place("c_late", [P, PACK, 384], F32, 130)
+        wgt_sb = place("wgt", [P, J], F32, 136)
+        wgt_cols = place("wgt_cols", [P, J], F32, 140)
+        wgt_rows = place("wgt_rows", [P, HALF], F32, 144)
+        ident = place("ident", [P, P], F32, 146)
+        bias = place("bias", [P, PACK], F32, 146.5)
+        warm = place("warm", [P, 2], F32, 146.75)
 
         def load_plane(n):
             nc.sync.dma_start(planes[n][:], rows(xT, n // PACK)[:, n % PACK, :])
 
-        def load_c(s):
-            j0, width = C_PIECES[s]
-            at = C_PIECES[s - 1][1] * (s % 2)
-            nc.sync.dma_start(c_raw[s // 2][:, :, at : at + width], rows(c, 0)[:, :, j0 : j0 + width])
-
-        wgt_rows = sb.tile([P, HALF], F32, name="wgt_rows", align_bytes=64)
         for d in range(2):
             nc.scalar.dma_start(wgt_rows[d:QUAD:2, :], wgt.rearrange("p (h c) -> (p h) c", h=2)[::WGT_STEP, :])
         nc.vector.memset(wgt_rows[QUAD : 2 * QUAD, :], 0.0)
         nc.vector.memset(wgt_rows[2 * QUAD :, :], 0.0)
-        nc.sync.dma_start(wt_raw[0], rows(wt, 0))
+        nc.sync.dma_start(wt_raw[0][:], rows(wt, 0))
         nc.sync.dma_start(offsets[:], offs)
-        load_plane(0)
-        load_plane(1)
-        load_plane(2)
-        load_plane(3)
-        nc.sync.dma_start(wt_raw[1], rows(wt, 1))
+        nc.sync.dma_start(wt_halves[0][:], rows(wt, 1)[:, :, : 2 * P])
+        for n in range(4):
+            load_plane(n)
+        nc.sync.dma_start(wt_halves[1][:], rows(wt, 1)[:, :, 2 * P :])
         load_plane(4)
         nc.sync.dma_start(wx_raw[:], rows(wx, 0))
         load_plane(5)
-        load_c(1)
-        load_c(0)
+        nc.sync.dma_start(c_early[:, :, :128], rows(c, 0)[:, :, :128])
+        nc.sync.dma_start(c_early[:, :, 128:], rows(c, 0)[:, :, 512:])
         load_plane(6)
         load_plane(7)
-        load_c(2)
+        nc.sync.dma_start(c_late[:], rows(c, 0)[:, :, LATE[0] : LATE[0] + LATE[1]])
         nc.sync.dma_start(bias[:], b.rearrange("(p t) -> p t", t=PACK))
 
-        warm = sb.tile([P, 2], F32, name="warm")
         nc.vector.memset(warm[:, 0:1], 0.0)
         nc.scalar.activation(warm[:, 1:2], warm[:, 0:1], GELU)
 
-        ident = sb.tile([P, P], F32, name="ident")
         make_identity(nc, ident[:])
-        eye = mx_tiles("eye", KP)
-        eye_bf = [staged_bf(J * i + FIRST // 2, KP // 2) for i in range(PACK)]
+        eye = mx_tiles("eye", KP, 147)
         for i in range(PACK):
-            nc.vector.memset(staged(J * i + FIRST // 2, KP // 2).bitcast(U32), 0)
-        for i in range(PACK):
-            nc.vector.tensor_copy(eye_bf[i].rearrange("p (m i) -> p m i", i=PACK)[:, :, i], ident[:])
-        for i in range(PACK):
-            quantize(eye, P * i, eye_bf[i])
+            eye_bf = place("eye_bf%d" % i, [P, KP], BF16, 72 + i)
+            nc.vector.memset(eye_bf[:].bitcast(U32), 0)
+            nc.vector.tensor_copy(eye_bf[:].rearrange("p (m i) -> p m i", i=PACK)[:, :, i], ident[:])
+            quantize(eye, P * i, eye_bf[:])
 
         def dealt(w_bf):
             return w_bf.rearrange("p (t m i) -> p m i t", t=PACK, i=PACK)
@@ -133,100 +126,6 @@ def tile_list_tier_geluP_kernel(tc, xT, wgt, wt, c, wx, b, offs, out_0, out_1, o
                 src.rearrange("p i (g r) -> p g i r", r=4),
             )
 
-        def picked_cols(a, j0, width):
-            return picked[a][:].rearrange("p (i j) -> p i j", i=PACK)[:, :, j0 : j0 + width]
-
-        def pick(n, j0, width):
-            at = J * n + j0
-            nc.vector.tensor_tensor(
-                staged(at, width),
-                planes[n][:].indirect(offsets[:, j0 // 16 : (j0 + width) // 16]),
-                wgt_sb[:, j0 : j0 + width],
-                ALU.mult,
-            )
-
-        def bank_tile(name, n):
-            return ps.tile([P, BANK], F32, name=name, tag="bank%d" % n)
-
-        xg = [mx_tiles("xg%d" % a, J) for a in range(2)]
-        wq = [mx_tiles("wq%d" % a, N) for a in range(2)]
-        wr = [mx_tiles("wr%d" % a, N) for a in range(2)]
-        wr_bfs = [sb.tile([P, N * PACK], BF16, name="wr_bf%d" % a, tag=("wr_bf0", "plane4")[a], align_bytes=64)[:] for a in range(2)]
-        xg0_both = sb.tile([P, J * PACK], BF16, name="xg0_both", align_bytes=64)
-        turned = [sb.tile([P, N * PACK], BF16, name="turned", align_bytes=64)[:]]
-        minus_q = [sb.tile([P, PACK * N], F32, name="minus_q", align_bytes=64)]
-        sums = [None]
-
-        def first_tier0():
-            w_bf = staged_bf(FIRST - 64, J)
-            for u in range(2):
-                nc.vector.tensor_copy(dealt(w_bf)[:, :, :, 2 * u : 2 * u + 2], by_slice(wt_raw[0])[:, :, :, 2 * u : 2 * u + 2])
-            quantize(wq[0], 0, w_bf)
-
-        def first_tier1():
-            for u in range(2):
-                w_bf = (xg0_both[:, 3 * N : 5 * N], wr_bfs[0][:, N : 3 * N])[u]
-                nc.scalar.copy(
-                    w_bf.rearrange("p (t m i) -> p m i t", t=2, i=PACK),
-                    by_slice(wt_raw[1])[:, :, :, 2 * u : 2 * (u + 1)],
-                )
-                quantize(wq[1], P * 2 * u, w_bf)
-
-        def second_tier1():
-            for q in range(4):
-                u, h = q // 2, q % 2
-                back = bank_tile("back1_%d" % q, 2 + q)
-                for i in range(PACK):
-                    for t2 in range(2):
-                        col = (t2 * PACK + i) * 64
-                        matmul(back[:, col : col + 64], eye, P * i, wq[1], P * (2 * u + t2) + 64 * h, True, True)
-                nc.vector.tensor_tensor(
-                    dealt(wr_bfs[1])[:, 64 * h : 64 * (h + 1), :, 2 * u : 2 * u + 2],
-                    by_slice(wt_raw[1])[:, 64 * h : 64 * (h + 1), :, 2 * u : 2 * u + 2],
-                    back[:].rearrange("p (t i m) -> p m i t", t=2, i=PACK),
-                    ALU.subtract,
-                )
-
-        def turn_weights(a):
-            sums[a] = [bank_tile("sum%d_%d" % (a, nb), PACK + nb) for nb in range(PACK)]
-            for nb in range(PACK):
-                for i in range(PACK):
-                    nc.tensor.matmul(sums[a][nb][:, P * i : P * (i + 1)], wt_raw[a][:, i, P * nb : P * (nb + 1)], ident[:],
-                                     start=(i == 0), stop=False, is_transpose=True)
-
-        def take_first_tier(a):
-            backs = [bank_tile("back%d_%d" % (a, i), i) for i in range(PACK)]
-            for i, back in enumerate(backs):
-                matmul(back[:], eye, P * i, wq[a], 0, True, True)
-            turn_weights(a)
-            for h in (1, 0):
-                for i, back in enumerate(backs):
-                    at = N * i + 2 * P * h
-                    nc.scalar.activation(minus_q[a][:, at : at + 2 * P].rearrange("p (m t) -> p m t", t=PACK),
-                                         back[:].rearrange("p (t m) -> p m t", t=PACK)[:, 64 * h : 64 * (h + 1), :], COPY, scale=-1.0)
-                    for nb in range(2 * h, 2 * h + 2):
-                        nc.tensor.matmul(sums[a][nb][:, P * i : P * (i + 1)], minus_q[a][:, N * i + P * nb : N * i + P * (nb + 1)], ident[:],
-                                         start=False, stop=(i == PACK - 1), is_transpose=True)
-
-        def round_residual(a):
-            for nb in (2, 3, 0, 1):
-                nc.scalar.copy(turned[a][:, KP * nb : KP * (nb + 1)].rearrange("n (u p e) -> n u p e", u=2, e=2),
-                               sums[a][nb][:].rearrange("n (u e p) -> n u p e", u=2, e=2))
-
-        def turn_back(a):
-            for h in range(2):
-                words = bank_tile("words%d_%d" % (a, h), h)
-                for nb2 in range(2):
-                    for u in range(2):
-                        at = 2 * P * (2 * h + nb2) + P * u
-                        nc.tensor.transpose(words[:, P * (2 * nb2 + u) : P * (2 * nb2 + u + 1)], turned[a].bitcast(F32)[:, at : at + P], ident[:])
-                nc.scalar.copy(
-                    wr_bfs[a].bitcast(F32).rearrange("p (t h b m u) -> p h t b m u", t=PACK, h=2, b=2, u=2)[:, h],
-                    words[:].rearrange("p (b u m t) -> p t b m u", b=2, u=2, t=PACK),
-                )
-            quantize(wr[a], 0, wr_bfs[a])
-
-        wgt_cols = sb.tile([P, J], F32, name="wgt_cols", align_bytes=64)
         across = [bank_tile("across%d" % v, 6 + v) for v in range(2)]
         for s in range(PACK):
             nc.tensor.transpose(across[s // 2][:, P * (s % 2) : P * (s % 2 + 1)], wgt_rows[:, P * s : P * (s + 1)], ident[:])
@@ -242,97 +141,195 @@ def tile_list_tier_geluP_kernel(tc, xT, wgt, wt, c, wx, b, offs, out_0, out_1, o
             for s in range(PACK):
                 nc.tensor.transpose(spread[:, P * s : P * (s + 1)], wgt_cols[:, HALF * h + P * s : HALF * h + P * (s + 1)], ident[:])
             nc.scalar.copy(wgt_sb[:, HALF * h : HALF * (h + 1)], spread[:])
-        first_tier0()
-        take_first_tier(0)
-        pick(0, 0, FIRST)
-        pick(0, FIRST, J - FIRST)
-        round_residual(0)
-        pick(1, 0, J)
-        pick(2, 0, J)
-        pick(3, 0, J)
-        first_tier1()
+
+        wq0 = mx_tiles("wq0", N, 150)
+        w_bf0 = place("w_bf0", [P, N * PACK], BF16, 69)
+        for u in range(2):
+            nc.vector.tensor_copy(dealt(w_bf0[:])[:, :, :, 2 * u : 2 * u + 2], by_slice(wt_raw[0][:])[:, :, :, 2 * u : 2 * u + 2])
+        quantize(wq0, 0, w_bf0[:])
+        wq = [wq0, mx_tiles("wq1", N, 152.5)]
+        w_bf1 = [place("w_bf1_%d" % u, [P, 2 * N], BF16, 70 - 2 * u) for u in range(2)]
+
+        def deal_half(copy, u, h):
+            copy(
+                w_bf1[u][:].rearrange("p (t m i) -> p m i t", t=2, i=PACK)[:, 64 * h : 64 * (h + 1)],
+                by_slice(wt_halves[h][:])[:, :, :, 2 * u : 2 * u + 2],
+            )
+
+        for u in range(2):
+            deal_half(nc.vector.tensor_copy, u, 0)
+
+        minus_q = place("minus_q", [P, PACK * N], F32, 155)
+        turned = place("turned", [P, N * PACK], BF16, 165)
+        wr_bf = [None, None]
+
+        backs, sums = {}, {}
+
+        def first_tier_back(a):
+            for i in range(PACK):
+                backs[a, i] = bank_tile("back%d_%d" % (a, i), i)
+                matmul(backs[a, i][:], eye, P * i, wq[a], 0, True, True)
+
+        def turn_weights(a, h):
+            for nb in (2 * h, 2 * h + 1):
+                sums[a, nb] = bank_tile("sum%d_%d" % (a, nb), PACK + nb)
+                for i in range(PACK):
+                    nc.tensor.matmul(sums[a, nb][:, P * i : P * (i + 1)], wt_raw[a][:, i, P * nb : P * (nb + 1)], ident[:],
+                                     start=(i == 0), stop=False, is_transpose=True)
+
+        def take_away(a, h):
+            for i in range(PACK):
+                at = N * i + 2 * P * h
+                nc.scalar.activation(minus_q[:, at : at + 2 * P].rearrange("p (m t) -> p m t", t=PACK),
+                                     backs[a, i][:].rearrange("p (t m) -> p m t", t=PACK)[:, 64 * h : 64 * (h + 1), :], COPY, scale=-1.0)
+                for nb in (2 * h, 2 * h + 1):
+                    nc.tensor.matmul(sums[a, nb][:, P * i : P * (i + 1)], minus_q[:, N * i + P * nb : N * i + P * (nb + 1)], ident[:],
+                                     start=False, stop=(i == PACK - 1), is_transpose=True)
+
+        def round_left(a, h):
+            for nb in (2 * h, 2 * h + 1):
+                nc.scalar.copy(turned[:, KP * nb : KP * (nb + 1)].rearrange("n (u p e) -> n u p e", u=2, e=2),
+                               sums[a, nb][:].rearrange("n (u e p) -> n u p e", u=2, e=2))
+
+        def turn_back(a, first_bank):
+            for h in (1, 0):
+                words = bank_tile("words%d_%d" % (a, h), first_bank + 1 - h)
+                for nb2 in range(2):
+                    for u in range(2):
+                        at = 2 * P * (2 * h + nb2) + P * u
+                        nc.tensor.transpose(words[:, P * (2 * nb2 + u) : P * (2 * nb2 + u + 1)], turned[:].bitcast(F32)[:, at : at + P], ident[:])
+                nc.scalar.copy(
+                    wr_bf[a][:].bitcast(F32).rearrange("p (t h b m u) -> p h t b m u", t=PACK, h=2, b=2, u=2)[:, h],
+                    words[:].rearrange("p (b u m t) -> p t b m u", b=2, u=2, t=PACK),
+                )
+
+        first_tier_back(0)
+        for h in (1, 0):
+            turn_weights(0, h)
+        for h in (1, 0):
+            take_away(0, h)
+        for h in (1, 0):
+            round_left(0, h)
+
+        picked = [place("picked%d" % a, [P, PACK, J], F32, 72 + 16 * a) for a in range(2)]
+
+        def pick(n, j0, width):
+            nc.vector.tensor_tensor(
+                picked[n // PACK][:, n % PACK, j0 : j0 + width],
+                planes[n][:].indirect(offsets[:, j0 // 16 : (j0 + width) // 16]),
+                wgt_sb[:, j0 : j0 + width],
+                ALU.mult,
+            )
+
+        for h in range(2):
+            pick(0, HALF * h, HALF)
+        for n in range(1, PACK):
+            pick(n, 0, J)
+        for u in range(2):
+            deal_half(nc.scalar.copy, u, 1)
+            quantize(wq[1], 2 * P * u, w_bf1[u][:])
         pick(4, 0, J)
-        turn_back(0)
-        second_tier1()
-        wxq = mx_tiles("wx", N)
-        wx_bf = sb.tile([P, N * PACK], BF16, name="wx_bf", align_bytes=64)
-        xg0_bf = (xg0_both[:, : 2 * J], xg0_both[:, 2 * J :])
-        c_both = [sb.tile([P, 640 * PACK], BF16, name="c_bf%d" % h, tag="plane%d" % h, align_bytes=64) for h in range(2)]
-        c_bf = [c_both[0][:, : PACK * 512], c_both[0][:, PACK * 512 :], c_both[1][:, PACK * 128 : PACK * 384], c_both[1][:, : PACK * 128]]
-        cq = mx_tiles("c", J)
+        wr_bf[0] = place("wr_bf0", [P, N * PACK], BF16, 66)
+        turn_back(0, 0)
+        wr = [mx_tiles("wr0", N, 171), mx_tiles("wr1", N, 24)]
+        quantize(wr[0], 0, wr_bf[0][:])
+        wr_bf[1] = place("wr_bf1", [P, N * PACK], BF16, 32)
+        for q in range(4):
+            u, h = q // 2, q % 2
+            back = bank_tile("back1_%d" % q, 2 + q)
+            for i in range(PACK):
+                for t2 in range(2):
+                    col = (t2 * PACK + i) * 64
+                    matmul(back[:, col : col + 64], eye, P * i, wq[1], P * (2 * u + t2) + 64 * h, True, True)
+            nc.vector.tensor_tensor(
+                dealt(wr_bf[1][:])[:, 64 * h : 64 * (h + 1), :, 2 * u : 2 * u + 2],
+                by_slice(wt_halves[h][:])[:, :, :, 2 * u : 2 * u + 2],
+                back[:].rearrange("p (t i m) -> p m i t", t=2, i=PACK),
+                ALU.subtract,
+            )
         pick(5, 0, J)
-        weave(nc.scalar.copy, xg0_bf[0], picked_cols(0, 0, HALF))
-        quantize(xg[0], 0, xg0_bf[0])
-        quantize(wr[1], 0, wr_bfs[1])
-        weave(nc.scalar.copy, xg0_bf[1], picked_cols(0, HALF, HALF))
-        quantize(xg[0], HALF, xg0_bf[1])
+        xg0_bf = [place("xg0_bf%d" % h, [P, HALF * PACK], BF16, 163 + 4 * h) for h in range(2)]
+        xg0 = [mx_tiles("xg0a", HALF, 155), mx_tiles("xg0b", HALF, 157.5)]
+        weave(nc.scalar.copy, xg0_bf[0][:], picked[0][:, :, :HALF])
+        quantize(xg0[0], 0, xg0_bf[0][:])
+        quantize(wr[1], 0, wr_bf[1][:])
+        weave(nc.scalar.copy, xg0_bf[1][:], picked[0][:, :, HALF:])
+        quantize(xg0[1], 0, xg0_bf[1][:])
+
+        wx_bf = place("wx_bf", [P, N * PACK], BF16, 175)
         nc.scalar.copy(dealt(wx_bf[:]), by_slice(wx_raw[:]))
-        quantize(wxq, 0, wx_bf[:])
-        weave(nc.scalar.copy, c_both[0][:], c_raw[0][:])
-        for s in range(2):
-            quantize(cq, C_PIECES[s][0], c_bf[s])
-        xg1_bf = sb.tile([P, J * PACK], BF16, name="xg1_bf", tag="c_raw0", align_bytes=64)
+        ce_bf = place("ce_bf", [P, 640 * PACK], BF16, 191)
+        weave(nc.scalar.copy, ce_bf[:], c_early[:])
+        xg1_bf = place("xg1_bf", [P, J * PACK], BF16, 120)
+
+        def xg1_cols(j0, width):
+            return xg1_bf[:, PACK * j0 : PACK * (j0 + width)]
 
         def weave_pair(copy, pair, j0, width):
             copy(
-                xg1_bf[:, PACK * j0 : PACK * (j0 + width)].rearrange("p (j i) -> p j i", i=PACK)[:, :, 2 * pair : 2 * pair + 2],
-                picked_cols(1, j0, width)[:, 2 * pair : 2 * pair + 2, :].rearrange("p i j -> p j i"),
+                xg1_cols(j0, width).rearrange("p (j i) -> p j i", i=PACK)[:, :, 2 * pair : 2 * pair + 2],
+                picked[1][:, 2 * pair : 2 * pair + 2, j0 : j0 + width].rearrange("p i j -> p j i"),
             )
 
-        weave_pair(nc.scalar.copy, 0, 0, J)
+        on_s, on_v = nc.scalar.copy, nc.vector.tensor_copy
+        for j0, width in EARLY + (LATE,):
+            weave_pair(on_s, 0, j0, width)
+        wxq = mx_tiles("wx", N, 160)
+        quantize(wxq, 0, wx_bf[:])
         pick(6, 0, J)
+        cq = (mx_tiles("ce", 640, 224), mx_tiles("cl", 384, 179))
+        quantize(cq[0], 0, ce_bf[:, : PACK * 128])
+        quantize(cq[0], 128, ce_bf[:, PACK * 128 :])
 
         acc = []
         first_bank = 0
         for j0, width in CHUNKS:
             nb = width * PACK // BANK
-            acc.append([ps.tile([P, BANK], F32, name="acc%d" % (first_bank + n), tag="bank%d" % (first_bank + n)) for n in range(nb)])
+            acc.append([bank_tile("acc%d" % (first_bank + n), first_bank + n) for n in range(nb)])
             first_bank = first_bank + nb
 
         def passes(ci, pairs, opens, closes):
-            j0, width = CHUNKS[ci]
+            width = CHUNKS[ci][1]
             per_bank = BANK // width
             for n, bank in enumerate(acc[ci]):
-                for s, (lhs, rhs) in enumerate(pairs):
+                for s, (lhs, rhs, col) in enumerate(pairs):
                     for r in range(per_bank):
                         t = n * per_bank + r
-                        matmul(bank[:, r * width : (r + 1) * width], lhs, P * t, rhs, j0,
+                        matmul(bank[:, r * width : (r + 1) * width], lhs, P * t, rhs, col,
                                opens and s == 0 and r == 0, closes and s == len(pairs) - 1 and r == per_bank - 1)
 
-        for ci in range(len(CHUNKS)):
-            passes(ci, [(wq[0], xg[0]), (wr[0], xg[0])], True, False)
+        for ci in (0, 3, 4, 1, 2):
+            j0 = CHUNKS[ci][0]
+            passes(ci, [(wq[0], xg0[j0 // HALF], j0 % HALF), (wr[0], xg0[j0 // HALF], j0 % HALF)], True, False)
         for ci in range(3):
-            passes(ci, [(wxq, cq)], False, False)
+            passes(ci, [(wxq, cq[0], max(CHUNKS[ci][0] - 384, 0))], False, False)
 
-        yq = mx_tiles("y", J)
+        xg1 = mx_tiles("xg1", J, 181)
+        yq = mx_tiles("y", J, 186)
         out_rows = out_0.rearrange("(p t) j -> p t j", t=PACK)
         out_words = out_1[0].rearrange("p j i -> p (j i)").bitcast(I32)
 
         def finish_sum(ci, copy):
             j0, width = CHUNKS[ci]
             weave_pair(copy, 1, j0, width)
-            quantize(xg[1], j0, xg1_bf[:, PACK * j0 : PACK * (j0 + width)])
-            passes(ci, [(wq[1], xg[1]), (wr[1], xg[1])], False, True)
+            quantize(xg1, j0, xg1_cols(j0, width))
+            passes(ci, [(wq[1], xg1, j0), (wr[1], xg1, j0)], False, True)
 
-        y_bf = sb.tile([P, J * PACK], BF16, name="y_bf", align_bytes=64)
-
+        y_bf = place("y_bf", [P, J * PACK], BF16, 204)
         ys = {}
 
-        def activate(chunks, copy, slot):
-            j0 = CHUNKS[chunks[0]][0]
-            span = sum(CHUNKS[ci][1] for ci in chunks)
-            y = sb.tile([P, PACK, span], F32, name="y%d" % chunks[0], tag=slot, align_bytes=64)
-            for ci in chunks:
-                at, width = CHUNKS[ci][0] - j0, CHUNKS[ci][1]
-                per_bank = BANK // width
-                for t in range(PACK):
-                    r = t % per_bank
-                    nc.scalar.activation(y[:, t, at : at + width], acc[ci][t // per_bank][:, r * width : (r + 1) * width], GELU, bias=bias[:, t : t + 1])
-                    if r == per_bank - 1:
-                        nc.sync.dma_start(out_rows[:, t - r : t + 1, j0 : j0 + span], y[:, t - r : t + 1, :])
-            ys[chunks[0]] = y
+        def activate(ci, copy):
+            j0, width = CHUNKS[ci]
+            y = place("y%d" % ci, [P, PACK, width], F32, (0, 4, 8, 12, 24)[ci])
+            per_bank = BANK // width
+            for t in range(PACK):
+                r = t % per_bank
+                nc.scalar.activation(y[:, t, :], acc[ci][t // per_bank][:, r * width : (r + 1) * width], GELU, bias=bias[:, t : t + 1])
+                if r == per_bank - 1:
+                    nc.sync.dma_start(out_rows[:, t - r : t + 1, j0 : j0 + width], y[:, t - r : t + 1, :])
+            ys[ci] = y
             if copy is not None:
-                weave_y(chunks[0], copy)
+                weave_y(ci, copy)
 
         def weave_y(ci, copy):
             j0, width = CHUNKS[ci]
@@ -344,29 +341,29 @@ def tile_list_tier_geluP_kernel(tc, xT, wgt, wt, c, wx, b, offs, out_0, out_1, o
         def store_words(j0, j1):
             nc.sync.dma_start(out_words[:, j0:j1], yq[0][:, j0:j1].bitcast(I32))
 
-        on_s, on_v = nc.scalar.copy, nc.vector.tensor_copy
         pick(7, *CHUNKS[0])
         finish_sum(0, on_v)
         pick(7, *CHUNKS[1])
         finish_sum(1, on_s)
         pick(7, *CHUNKS[2])
         finish_sum(2, on_s)
-        pick(7, *C_PIECES[2])
-        weave(on_v, c_both[1][:, : PACK * 384], c_raw[1][:])
-        for s in (2, 3):
-            quantize(cq, CHUNKS[s + 1][0], c_bf[s])
-        passes(3, [(wxq, cq)], False, False)
-        passes(4, [(wxq, cq)], False, False)
+        pick(7, *LATE)
+        cl_bf = place("cl_bf", [P, 384 * PACK], BF16, 196)
+        weave(on_v, cl_bf[:], c_late[:])
+        quantize(cq[1], 128, cl_bf[:, PACK * 128 :])
+        quantize(cq[1], 0, cl_bf[:, : PACK * 128])
+        passes(3, [(wxq, cq[1], 128)], False, False)
+        passes(4, [(wxq, cq[1], 0)], False, False)
         finish_sum(3, on_v)
         finish_sum(4, on_v)
-        activate([0], None, "plane0")
-        activate([1], on_v, "plane5")
-        activate([2], on_v, "plane2")
+        activate(0, None)
+        activate(1, on_v)
+        activate(2, on_v)
         quantize_y(512, 1024)
-        activate([3], on_v, "plane3")
+        activate(3, on_v)
         store_words(512, 1024)
         quantize_y(256, 512)
-        activate([4], None, "y4")
+        activate(4, None)
         weave_y(0, on_s)
         quantize_y(0, 128)
         weave_y(4, on_v)

@@ -71,7 +71,7 @@ def tile_list_tier_geluP_kernel(tc, xT, wgt, wt, c, wx, b, offs, out_0, out_1, o
         wt_raw = [place("wt_raw0", [P, PACK, N], F32, 216)]
         wt_halves = [place("wt_half%d" % h, [P, PACK, 2 * P], F32, 104 + 4 * h) for h in range(2)]
         wx_raw = place("wx_raw", [P, PACK, N], F32, 112)
-        c_early = place("c_early", [P, PACK, 640], F32, 120)
+        c_early = [place("c_early0", [P, PACK, 128], F32, 128), place("c_early1", [P, PACK, HALF], F32, 120)]
         c_late = place("c_late", [P, PACK, 384], F32, 130)
         wgt_sb = place("wgt", [P, J], F32, 136)
         wgt_cols = place("wgt_cols", [P, J], F32, 140)
@@ -96,8 +96,8 @@ def tile_list_tier_geluP_kernel(tc, xT, wgt, wt, c, wx, b, offs, out_0, out_1, o
         load_plane(4)
         nc.sync.dma_start(wx_raw[:], rows(wx, 0))
         load_plane(5)
-        nc.sync.dma_start(c_early[:, :, :128], rows(c, 0)[:, :, :128])
-        nc.sync.dma_start(c_early[:, :, 128:], rows(c, 0)[:, :, 512:])
+        nc.sync.dma_start(c_early[0][:], rows(c, 0)[:, :, :128])
+        nc.sync.dma_start(c_early[1][:], rows(c, 0)[:, :, 512:])
         load_plane(6)
         load_plane(7)
         nc.sync.dma_start(c_late[:], rows(c, 0)[:, :, LATE[0] : LATE[0] + LATE[1]])
@@ -161,7 +161,7 @@ def tile_list_tier_geluP_kernel(tc, xT, wgt, wt, c, wx, b, offs, out_0, out_1, o
 
         minus_q = place("minus_q", [P, PACK * N], F32, 155)
         turned = place("turned", [P, N * PACK], BF16, 165)
-        wr_bf = [None, None]
+        wr_bf = [place("wr_bf0", [P, N * PACK], BF16, 171), None]
 
         backs, sums = {}, {}
 
@@ -210,6 +210,7 @@ def tile_list_tier_geluP_kernel(tc, xT, wgt, wt, c, wx, b, offs, out_0, out_1, o
             take_away(0, h)
         for h in (1, 0):
             round_left(0, h)
+        turn_back(0, 0)
 
         picked = [place("picked%d" % a, [P, PACK, J], F32, 72 + 16 * a) for a in range(2)]
 
@@ -228,11 +229,9 @@ def tile_list_tier_geluP_kernel(tc, xT, wgt, wt, c, wx, b, offs, out_0, out_1, o
         for u in range(2):
             deal_half(nc.scalar.copy, u, 1)
             quantize(wq[1], 2 * P * u, w_bf1[u][:])
-        pick(4, 0, J)
-        wr_bf[0] = place("wr_bf0", [P, N * PACK], BF16, 66)
-        turn_back(0, 0)
-        wr = [mx_tiles("wr0", N, 171), mx_tiles("wr1", N, 24)]
+        wr = [(place("wr0_codes", [P, N], U32, 64), place("wr0_scales", [P, N], U8, 68)), None]
         quantize(wr[0], 0, wr_bf[0][:])
+        pick(4, 0, J)
         wr_bf[1] = place("wr_bf1", [P, N * PACK], BF16, 32)
         for q in range(4):
             u, h = q // 2, q % 2
@@ -249,17 +248,20 @@ def tile_list_tier_geluP_kernel(tc, xT, wgt, wt, c, wx, b, offs, out_0, out_1, o
             )
         pick(5, 0, J)
         xg0_bf = [place("xg0_bf%d" % h, [P, HALF * PACK], BF16, 163 + 4 * h) for h in range(2)]
-        xg0 = [mx_tiles("xg0a", HALF, 155), mx_tiles("xg0b", HALF, 157.5)]
+        xg0 = [mx_tiles("xg0a", HALF, 155), None]
         weave(nc.scalar.copy, xg0_bf[0][:], picked[0][:, :, :HALF])
         quantize(xg0[0], 0, xg0_bf[0][:])
-        quantize(wr[1], 0, wr_bf[1][:])
         weave(nc.scalar.copy, xg0_bf[1][:], picked[0][:, :, HALF:])
-        quantize(xg0[1], 0, xg0_bf[1][:])
 
         wx_bf = place("wx_bf", [P, N * PACK], BF16, 175)
         nc.scalar.copy(dealt(wx_bf[:]), by_slice(wx_raw[:]))
         ce_bf = place("ce_bf", [P, 640 * PACK], BF16, 191)
-        weave(nc.scalar.copy, ce_bf[:], c_early[:])
+        weave(nc.scalar.copy, ce_bf[:, : PACK * 128], c_early[0][:])
+        xg0[1] = (place("xg0b_codes", [P, HALF], U32, 157.5), place("xg0b_scales", [P, HALF], U8, 128))
+        wr[1] = (place("wr1_codes", [P, N], U32, 24), place("wr1_scales", [P, N], U8, 128.5))
+        quantize(wr[1], 0, wr_bf[1][:])
+        quantize(xg0[1], 0, xg0_bf[1][:])
+        weave(nc.scalar.copy, ce_bf[:, PACK * 128 :], c_early[1][:])
         xg1_bf = place("xg1_bf", [P, J * PACK], BF16, 120)
 
         def xg1_cols(j0, width):

@@ -69,12 +69,12 @@ def tile_list_tier_geluP_kernel(tc, xT, wgt, wt, c, wx, b, offs, out_0, out_1, o
         offsets = held.tile([P, J // 16], U16, name="offsets")
         planes = [place("plane%d" % n, [P, T], F32, 8 * n) for n in range(2 * PACK)]
         wt_raw = [place("wt_raw0", [P, PACK, N], F32, 216)]
-        wt_halves = [place("wt_half%d" % h, [P, PACK, 2 * P], F32, 104 + 4 * h) for h in range(2)]
+        wt_halves = [place("wt_half%d" % h, [P, PACK, 2 * P], F32, 228 + 4 * h) for h in range(2)]
         wx_raw = place("wx_raw", [P, PACK, N], F32, 112)
         c_early = [place("c_early0", [P, PACK, 128], F32, 128), place("c_early1", [P, PACK, HALF], F32, 120)]
         c_late = place("c_late", [P, PACK, 384], F32, 130)
         wgt_sb = place("wgt", [P, J], F32, 136)
-        wgt_cols = place("wgt_cols", [P, J], F32, 140)
+        wgt_cols = [place("wgt_cols%d" % q, [P, 2 * P], F32, 140 + q) for q in range(PACK)]
         wgt_rows = place("wgt_rows", [P, HALF], F32, 144)
         ident = place("ident", [P, P], F32, 146)
         bias = place("bias", [P, PACK], F32, 146.5)
@@ -89,14 +89,14 @@ def tile_list_tier_geluP_kernel(tc, xT, wgt, wt, c, wx, b, offs, out_0, out_1, o
         nc.vector.memset(wgt_rows[2 * QUAD :, :], 0.0)
         nc.sync.dma_start(wt_raw[0][:], rows(wt, 0))
         nc.sync.dma_start(offsets[:], offs)
-        nc.sync.dma_start(wt_halves[0][:], rows(wt, 1)[:, :, : 2 * P])
         for n in range(4):
             load_plane(n)
-        nc.sync.dma_start(wt_halves[1][:], rows(wt, 1)[:, :, 2 * P :])
+        nc.sync.dma_start(wt_halves[0][:], rows(wt, 1)[:, :, : 2 * P])
         load_plane(4)
-        nc.sync.dma_start(wx_raw[:], rows(wx, 0))
-        load_plane(5)
+        nc.sync.dma_start(wt_halves[1][:], rows(wt, 1)[:, :, 2 * P :])
         nc.sync.dma_start(c_early[0][:], rows(c, 0)[:, :, :128])
+        load_plane(5)
+        nc.sync.dma_start(wx_raw[:], rows(wx, 0))
         nc.sync.dma_start(c_early[1][:], rows(c, 0)[:, :, 512:])
         load_plane(6)
         load_plane(7)
@@ -129,18 +129,25 @@ def tile_list_tier_geluP_kernel(tc, xT, wgt, wt, c, wx, b, offs, out_0, out_1, o
         across = [bank_tile("across%d" % v, 6 + v) for v in range(2)]
         for s in range(PACK):
             nc.tensor.transpose(across[s // 2][:, P * (s % 2) : P * (s % 2 + 1)], wgt_rows[:, P * s : P * (s + 1)], ident[:])
-        for h in range(2):
-            for v in range(2):
-                at = HALF * h + 2 * P * v
-                nc.scalar.copy(
-                    wgt_cols[:, at : at + 2 * P].rearrange("c (s g d r) -> c s g d r", s=2, g=GROUPS, d=2),
-                    across[v][:, : 2 * P].rearrange("c (s z g h d) -> c s z g h d", s=2, g=GROUPS, h=2, d=2)[:, :, 0, :, h, :].unsqueeze(4).to_broadcast([P, 2, GROUPS, 2, GROUPS]),
-                )
-        for h in range(2):
-            spread = bank_tile("spread%d" % h, 4 + h)
-            for s in range(PACK):
-                nc.tensor.transpose(spread[:, P * s : P * (s + 1)], wgt_cols[:, HALF * h + P * s : HALF * h + P * (s + 1)], ident[:])
-            nc.scalar.copy(wgt_sb[:, HALF * h : HALF * (h + 1)], spread[:])
+
+        def repeat_quarter(q):
+            h, v = q // 2, q % 2
+            nc.scalar.copy(
+                wgt_cols[q][:].rearrange("c (s g d r) -> c s g d r", s=2, g=GROUPS, d=2),
+                across[v][:, : 2 * P].rearrange("c (s z g h d) -> c s z g h d", s=2, g=GROUPS, h=2, d=2)[:, :, 0, :, h, :].unsqueeze(4).to_broadcast([P, 2, GROUPS, 2, GROUPS]),
+            )
+
+        def spread_quarter(q):
+            spread = bank_tile("spread%d" % q, 4 + q % 2)
+            for s in range(2):
+                nc.tensor.transpose(spread[:, P * s : P * (s + 1)], wgt_cols[q][:, P * s : P * (s + 1)], ident[:])
+            nc.scalar.copy(wgt_sb[:, 2 * P * q : 2 * P * (q + 1)], spread[:, : 2 * P])
+
+        repeat_quarter(0)
+        for q in range(PACK):
+            if q + 1 < PACK:
+                repeat_quarter(q + 1)
+            spread_quarter(q)
 
         wq0 = mx_tiles("wq0", N, 150)
         w_bf0 = place("w_bf0", [P, N * PACK], BF16, 69)
@@ -148,7 +155,7 @@ def tile_list_tier_geluP_kernel(tc, xT, wgt, wt, c, wx, b, offs, out_0, out_1, o
             nc.vector.tensor_copy(dealt(w_bf0[:])[:, :, :, 2 * u : 2 * u + 2], by_slice(wt_raw[0][:])[:, :, :, 2 * u : 2 * u + 2])
         quantize(wq0, 0, w_bf0[:])
         wq = [wq0, mx_tiles("wq1", N, 152.5)]
-        w_bf1 = [place("w_bf1_%d" % u, [P, 2 * N], BF16, 70 - 2 * u) for u in range(2)]
+        w_bf1 = [place("w_bf1_%d" % u, [P, 2 * N], BF16, 167.5 - 2 * u) for u in range(2)]
 
         def deal_half(copy, u, h):
             copy(
@@ -156,12 +163,9 @@ def tile_list_tier_geluP_kernel(tc, xT, wgt, wt, c, wx, b, offs, out_0, out_1, o
                 by_slice(wt_halves[h][:])[:, :, :, 2 * u : 2 * u + 2],
             )
 
-        for u in range(2):
-            deal_half(nc.vector.tensor_copy, u, 0)
-
         minus_q = place("minus_q", [P, PACK * N], F32, 155)
         turned = place("turned", [P, N * PACK], BF16, 165)
-        wr_bf = [place("wr_bf0", [P, N * PACK], BF16, 171), None]
+        wr_bf = [place("wr_bf0", [P, N * PACK], BF16, 102), None]
 
         backs, sums = {}, {}
 
@@ -211,6 +215,8 @@ def tile_list_tier_geluP_kernel(tc, xT, wgt, wt, c, wx, b, offs, out_0, out_1, o
         for h in (1, 0):
             round_left(0, h)
         turn_back(0, 0)
+        for u in range(2):
+            deal_half(nc.scalar.copy, u, 0)
 
         picked = [place("picked%d" % a, [P, PACK, J], F32, 72 + 16 * a) for a in range(2)]
 
@@ -222,20 +228,28 @@ def tile_list_tier_geluP_kernel(tc, xT, wgt, wt, c, wx, b, offs, out_0, out_1, o
                 ALU.mult,
             )
 
-        for h in range(2):
-            pick(0, HALF * h, HALF)
+        for q in range(PACK):
+            pick(0, 2 * P * q, 2 * P)
         for n in range(1, PACK):
             pick(n, 0, J)
+        wr = [(place("wr0_codes", [P, N], U32, 16), place("wr0_scales", [P, N], U8, 18)), mx_tiles("wr1", N, 64)]
+        quantize(wr[0], 0, wr_bf[0][:])
+        pick(4, 0, J)
+        xg0_bf = [place("xg0_bf0", [P, HALF * PACK], BF16, 161.5), None]
+        weave(nc.scalar.copy, xg0_bf[0][:, : PACK * 384], picked[0][:, :, :384])
         for u in range(2):
             deal_half(nc.scalar.copy, u, 1)
             quantize(wq[1], 2 * P * u, w_bf1[u][:])
-        wr = [(place("wr0_codes", [P, N], U32, 64), place("wr0_scales", [P, N], U8, 68)), None]
-        quantize(wr[0], 0, wr_bf[0][:])
-        pick(4, 0, J)
-        wr_bf[1] = place("wr_bf1", [P, N * PACK], BF16, 32)
+        weave(nc.scalar.copy, xg0_bf[0][:, PACK * 384 :], picked[0][:, :, 384:HALF])
+        xg0 = [(place("xg0a_codes", [P, HALF], U32, 155), place("xg0a_scales", [P, HALF], U8, 165.5)), mx_tiles("xg0b", HALF, 157.5)]
+        quantize(xg0[0], 0, xg0_bf[0][:])
+        xg0_bf[1] = place("xg0_bf1", [P, HALF * PACK], BF16, 104)
+        weave(nc.scalar.copy, xg0_bf[1][:], picked[0][:, :, HALF:])
+        pick(5, 0, J)
+        wr_bf[1] = place("wr_bf1", [P, N * PACK], BF16, 40)
         for q in range(4):
             u, h = q // 2, q % 2
-            back = bank_tile("back1_%d" % q, 2 + q)
+            back = bank_tile("back1_%d" % q, 1 + q)
             for i in range(PACK):
                 for t2 in range(2):
                     col = (t2 * PACK + i) * 64
@@ -246,22 +260,16 @@ def tile_list_tier_geluP_kernel(tc, xT, wgt, wt, c, wx, b, offs, out_0, out_1, o
                 back[:].rearrange("p (t i m) -> p m i t", t=2, i=PACK),
                 ALU.subtract,
             )
-        pick(5, 0, J)
-        xg0_bf = [place("xg0_bf%d" % h, [P, HALF * PACK], BF16, 163 + 4 * h) for h in range(2)]
-        xg0 = [mx_tiles("xg0a", HALF, 155), None]
-        weave(nc.scalar.copy, xg0_bf[0][:], picked[0][:, :, :HALF])
-        quantize(xg0[0], 0, xg0_bf[0][:])
-        weave(nc.scalar.copy, xg0_bf[1][:], picked[0][:, :, HALF:])
-
+        quantize(xg0[1], 0, xg0_bf[1][:])
+        ce_bf = [place("ce_bf0", [P, 128 * PACK], BF16, 191), place("ce_bf1", [P, HALF * PACK], BF16, 192)]
+        weave(nc.scalar.copy, ce_bf[0][:], c_early[0][:])
+        c_first = mx_tiles("c_first", 128, 224)
+        quantize(c_first, 0, ce_bf[0][:])
+        for u in range(2):
+            quantize(wr[1], 2 * P * u, wr_bf[1][:, 2 * N * u : 2 * N * (u + 1)])
         wx_bf = place("wx_bf", [P, N * PACK], BF16, 175)
         nc.scalar.copy(dealt(wx_bf[:]), by_slice(wx_raw[:]))
-        ce_bf = place("ce_bf", [P, 640 * PACK], BF16, 191)
-        weave(nc.scalar.copy, ce_bf[:, : PACK * 128], c_early[0][:])
-        xg0[1] = (place("xg0b_codes", [P, HALF], U32, 157.5), place("xg0b_scales", [P, HALF], U8, 128))
-        wr[1] = (place("wr1_codes", [P, N], U32, 24), place("wr1_scales", [P, N], U8, 128.5))
-        quantize(wr[1], 0, wr_bf[1][:])
-        quantize(xg0[1], 0, xg0_bf[1][:])
-        weave(nc.scalar.copy, ce_bf[:, PACK * 128 :], c_early[1][:])
+        weave(nc.scalar.copy, ce_bf[1][:], c_early[1][:])
         xg1_bf = place("xg1_bf", [P, J * PACK], BF16, 120)
 
         def xg1_cols(j0, width):
@@ -279,9 +287,9 @@ def tile_list_tier_geluP_kernel(tc, xT, wgt, wt, c, wx, b, offs, out_0, out_1, o
         wxq = mx_tiles("wx", N, 160)
         quantize(wxq, 0, wx_bf[:])
         pick(6, 0, J)
-        cq = (mx_tiles("ce", 640, 224), mx_tiles("cl", 384, 179))
-        quantize(cq[0], 0, ce_bf[:, : PACK * 128])
-        quantize(cq[0], 128, ce_bf[:, PACK * 128 :])
+        c_wide = mx_tiles("c_wide", HALF, 225)
+        quantize(c_wide, 0, ce_bf[1][:])
+        c_last = mx_tiles("c_last", 384, 179)
 
         acc = []
         first_bank = 0
@@ -303,8 +311,9 @@ def tile_list_tier_geluP_kernel(tc, xT, wgt, wt, c, wx, b, offs, out_0, out_1, o
         for ci in (0, 3, 4, 1, 2):
             j0 = CHUNKS[ci][0]
             passes(ci, [(wq[0], xg0[j0 // HALF], j0 % HALF), (wr[0], xg0[j0 // HALF], j0 % HALF)], True, False)
-        for ci in range(3):
-            passes(ci, [(wxq, cq[0], max(CHUNKS[ci][0] - 384, 0))], False, False)
+        passes(0, [(wxq, c_first, 0)], False, False)
+        for ci in (1, 2):
+            passes(ci, [(wxq, c_wide, CHUNKS[ci][0] - HALF)], False, False)
 
         xg1 = mx_tiles("xg1", J, 181)
         yq = mx_tiles("y", J, 186)
@@ -352,10 +361,10 @@ def tile_list_tier_geluP_kernel(tc, xT, wgt, wt, c, wx, b, offs, out_0, out_1, o
         pick(7, *LATE)
         cl_bf = place("cl_bf", [P, 384 * PACK], BF16, 196)
         weave(on_v, cl_bf[:], c_late[:])
-        quantize(cq[1], 128, cl_bf[:, PACK * 128 :])
-        quantize(cq[1], 0, cl_bf[:, : PACK * 128])
-        passes(3, [(wxq, cq[1], 128)], False, False)
-        passes(4, [(wxq, cq[1], 0)], False, False)
+        quantize(c_last, 128, cl_bf[:, PACK * 128 :])
+        quantize(c_last, 0, cl_bf[:, : PACK * 128])
+        passes(3, [(wxq, c_last, 128)], False, False)
+        passes(4, [(wxq, c_last, 0)], False, False)
         finish_sum(3, on_v)
         finish_sum(4, on_v)
         activate(0, None)

@@ -94,10 +94,10 @@ def tile_list_tier_geluP_kernel(tc, xT, wgt, wt, c, wx, b, offs, out_0, out_1, o
         nc.sync.dma_start(wt_halves[0][:], rows(wt, 1)[:, :, : 2 * P])
         load_plane(4)
         nc.sync.dma_start(wt_halves[1][:], rows(wt, 1)[:, :, 2 * P :])
-        nc.sync.dma_start(c_early[0][:], rows(c, 0)[:, :, :128])
         load_plane(5)
         nc.sync.dma_start(wx_raw[:], rows(wx, 0))
         nc.sync.dma_start(c_early[1][:], rows(c, 0)[:, :, 512:])
+        nc.sync.dma_start(c_early[0][:], rows(c, 0)[:, :, :128])
         load_plane(6)
         load_plane(7)
         nc.sync.dma_start(c_late[:], rows(c, 0)[:, :, LATE[0] : LATE[0] + LATE[1]])
@@ -236,12 +236,12 @@ def tile_list_tier_geluP_kernel(tc, xT, wgt, wt, c, wx, b, offs, out_0, out_1, o
         quantize(wr[0], 0, wr_bf[0][:])
         pick(4, 0, J)
         xg0_bf = [place("xg0_bf0", [P, HALF * PACK], BF16, 161.5), None]
-        weave(nc.scalar.copy, xg0_bf[0][:, : PACK * 384], picked[0][:, :, :384])
+        weave(nc.scalar.copy, xg0_bf[0][:, : PACK * 256], picked[0][:, :, :256])
         for u in range(2):
             deal_half(nc.scalar.copy, u, 1)
             quantize(wq[1], 2 * P * u, w_bf1[u][:])
-        weave(nc.scalar.copy, xg0_bf[0][:, PACK * 384 :], picked[0][:, :, 384:HALF])
-        xg0 = [(place("xg0a_codes", [P, HALF], U32, 155), place("xg0a_scales", [P, HALF], U8, 165.5)), mx_tiles("xg0b", HALF, 157.5)]
+        weave(nc.scalar.copy, xg0_bf[0][:, PACK * 256 :], picked[0][:, :, 256:HALF])
+        xg0 = [(place("xg0a_codes", [P, HALF], U32, 155), place("xg0a_scales", [P, HALF], U8, 165.5)), None]
         quantize(xg0[0], 0, xg0_bf[0][:])
         xg0_bf[1] = place("xg0_bf1", [P, HALF * PACK], BF16, 104)
         weave(nc.scalar.copy, xg0_bf[1][:], picked[0][:, :, HALF:])
@@ -260,16 +260,13 @@ def tile_list_tier_geluP_kernel(tc, xT, wgt, wt, c, wx, b, offs, out_0, out_1, o
                 back[:].rearrange("p (t i m) -> p m i t", t=2, i=PACK),
                 ALU.subtract,
             )
-        quantize(xg0[1], 0, xg0_bf[1][:])
         ce_bf = [place("ce_bf0", [P, 128 * PACK], BF16, 191), place("ce_bf1", [P, HALF * PACK], BF16, 192)]
-        weave(nc.scalar.copy, ce_bf[0][:], c_early[0][:])
-        c_first = mx_tiles("c_first", 128, 224)
-        quantize(c_first, 0, ce_bf[0][:])
         for u in range(2):
             quantize(wr[1], 2 * P * u, wr_bf[1][:, 2 * N * u : 2 * N * (u + 1)])
         wx_bf = place("wx_bf", [P, N * PACK], BF16, 175)
         nc.scalar.copy(dealt(wx_bf[:]), by_slice(wx_raw[:]))
         weave(nc.scalar.copy, ce_bf[1][:], c_early[1][:])
+        weave(nc.scalar.copy, ce_bf[0][:], c_early[0][:])
         xg1_bf = place("xg1_bf", [P, J * PACK], BF16, 120)
 
         def xg1_cols(j0, width):
@@ -286,9 +283,13 @@ def tile_list_tier_geluP_kernel(tc, xT, wgt, wt, c, wx, b, offs, out_0, out_1, o
             weave_pair(on_s, 0, j0, width)
         wxq = mx_tiles("wx", N, 160)
         quantize(wxq, 0, wx_bf[:])
-        pick(6, 0, J)
+        xg0[1] = (place("xg0b_codes", [P, HALF], U32, 157.5), place("xg0b_scales", [P, HALF], U8, 175))
+        quantize(xg0[1], 0, xg0_bf[1][:])
         c_wide = mx_tiles("c_wide", HALF, 225)
         quantize(c_wide, 0, ce_bf[1][:])
+        pick(6, 0, J)
+        c_first = mx_tiles("c_first", 128, 224)
+        quantize(c_first, 0, ce_bf[0][:])
         c_last = mx_tiles("c_last", 384, 179)
 
         acc = []

@@ -239,17 +239,19 @@ def tile_list_tier_geluP_kernel(tc, xT, wgt, wt, c, wx, b, offs, out_0, out_1, o
         weave(nc.scalar.copy, xg0_bf[0][:, : PACK * 256], picked[0][:, :, :256])
         for u in range(2):
             deal_half(nc.scalar.copy, u, 1)
-            quantize(wq[1], 2 * P * u, w_bf1[u][:])
+        quantize(wq[1], 0, w_bf1[0][:])
+        xg0 = [(place("xg0a_codes", [P, HALF], U32, 155), place("xg0a_scales", [P, HALF], U8, 167.5)), None]
+        quantize(xg0[0], 0, xg0_bf[0][:, : PACK * 256])
+        quantize(wq[1], 2 * P, w_bf1[1][:])
         weave(nc.scalar.copy, xg0_bf[0][:, PACK * 256 :], picked[0][:, :, 256:HALF])
-        xg0 = [(place("xg0a_codes", [P, HALF], U32, 155), place("xg0a_scales", [P, HALF], U8, 165.5)), None]
-        quantize(xg0[0], 0, xg0_bf[0][:])
+        quantize(xg0[0], 256, xg0_bf[0][:, PACK * 256 :])
         xg0_bf[1] = place("xg0_bf1", [P, HALF * PACK], BF16, 104)
         weave(nc.scalar.copy, xg0_bf[1][:], picked[0][:, :, HALF:])
         pick(5, 0, J)
         wr_bf[1] = place("wr_bf1", [P, N * PACK], BF16, 40)
         for q in range(4):
             u, h = q // 2, q % 2
-            back = bank_tile("back1_%d" % q, 1 + q)
+            back = bank_tile("back1_%d" % q, (0, 7, 1, 2)[q])
             for i in range(PACK):
                 for t2 in range(2):
                     col = (t2 * PACK + i) * 64
@@ -309,7 +311,7 @@ def tile_list_tier_geluP_kernel(tc, xT, wgt, wt, c, wx, b, offs, out_0, out_1, o
                         matmul(bank[:, r * width : (r + 1) * width], lhs, P * t, rhs, col,
                                opens and s == 0 and r == 0, closes and s == len(pairs) - 1 and r == per_bank - 1)
 
-        for ci in (0, 3, 4, 1, 2):
+        for ci in (3, 0, 4, 2, 1):
             j0 = CHUNKS[ci][0]
             passes(ci, [(wq[0], xg0[j0 // HALF], j0 % HALF), (wr[0], xg0[j0 // HALF], j0 % HALF)], True, False)
         passes(0, [(wxq, c_first, 0)], False, False)

from contextlib import ExitStack

import concourse.mybir as mybir
from concourse.masks import make_identity

K, L, N, T, J = 1024, 512, 512, 2048, 1024
FLOPS = 3221225472

F32 = mybir.dt.float32
BF16 = mybir.dt.bfloat16
U32 = mybir.dt.uint32
I32 = mybir.dt.int32
U16 = mybir.dt.uint16
U8 = mybir.dt.uint8
FP8X4 = mybir.dt.float8_e4m3fn_x4
ALU = mybir.AluOpType
GELU = mybir.ActivationFunctionType.Gelu_apprx_tanh
COPY = mybir.ActivationFunctionType.Copy

P = 128
PACK = 4
KP = P * PACK
HALF = 512
BANK = 512
GROUPS = 8
QUAD = 32
WGT_STEP = 17
KIB = 1024
CHUNKS = ((0, 128), (512, 256), (768, 256), (256, 256), (128, 128))
EARLY = ((0, 128), (512, 512))
LATE = (128, 384)


def tile_list_tier_geluP_kernel(tc, xT, wgt, wt, c, wx, b, offs, out_0, out_1, out_2):
    nc = tc.nc
    with ExitStack() as ctx:
        held = ctx.enter_context(tc.tile_pool(name="held", bufs=1))
        sb = ctx.enter_context(tc.tile_pool(name="sb", bufs=1))
        ps = ctx.enter_context(tc.psum_pool(name="ps", bufs=1))

        def place(name, shape, dtype, kib):
            return sb.tile(shape, dtype, name=name, align_bytes=64, offset=int(kib * KIB))

        def mx_tiles(name, width, kib):
            return place(name + "_codes", [P, width], U32, kib), place(name + "_scales", [P, width], U8, kib + width * 4 / KIB)

        def quantize(dst, col, src):
            width = src.shape[1] // PACK
            nc.vector.quantize_mx(out=dst[0][:, col : col + width].bitcast(FP8X4), scales=dst[1][:, col : col + width], in_=src)

        def matmul(out, lhs, lcol, rhs, rcol, start, stop):
            width = out.shape[1]
            nc.tensor.matmul_mx(
                out=out,
                lhsT=lhs[0][:, lcol : lcol + P].bitcast(FP8X4),
                lhsT_scale=lhs[1][:, lcol : lcol + P],
                rhs=rhs[0][:, rcol : rcol + width].bitcast(FP8X4),
                rhs_scale=rhs[1][:, rcol : rcol + width],
                start=start,
                stop=stop,
            )

        def rows(src, a):
            return src[KP * a : KP * (a + 1), :].rearrange("(p i) w -> p i w", i=PACK)

        def bank_tile(name, n):
            return ps.tile([P, BANK], F32, name=name, tag="bank%d" % n)

        offsets = held.tile([P, J // 16], U16, name="offsets")
        planes = [place("plane%d" % n, [P, T], F32, 8 * n) for n in range(2 * PACK)]
        wt_raw = [place("wt_raw0", [P, PACK, N], F32, 216)]
        wt_halves = [place("wt_half%d" % h, [P, PACK, 2 * P], F32, 228 + 4 * h) for h in range(2)]
        wx_raw = place("wx_raw", [P, PACK, N], F32, 112)
        c_early = [place("c_early0", [P, PACK, 128], F32, 128), place("c_early1", [P, PACK, HALF], F32, 120)]
        c_late = place("c_late", [P, PACK, 384], F32, 130)
        wgt_sb = place("wgt", [P, J], F32, 136)
        wgt_cols = [place("wgt_cols%d" % q, [P, 2 * P], F32, 140 + q) for q in range(PACK)]
        wgt_rows = place("wgt_rows", [P, HALF], F32, 144)
        ident = place("ident", [P, P], F32, 146)
        bias = place("bias", [P, PACK], F32, 146.5)
        warm = place("warm", [P, 2], F32, 146.75)

        def load_plane(n):
            nc.sync.dma_start(planes[n][:], rows(xT, n // PACK)[:, n % PACK, :])

        for d in range(2):
            nc.scalar.dma_start(wgt_rows[d:QUAD:2, :], wgt.rearrange("p (h c) -> (p h) c", h=2)[::WGT_STEP, :])
        nc.vector.memset(wgt_rows[QUAD : 2 * QUAD, :], 0.0)
        nc.vector.memset(wgt_rows[2 * QUAD :, :], 0.0)
        nc.sync.dma_start(wt_raw[0][:], rows(wt, 0))
        nc.sync.dma_start(offsets[:], offs)
        for n in range(4):
            load_plane(n)
        nc.sync.dma_start(wt_halves[0][:], rows(wt, 1)[:, :, : 2 * P])
        load_plane(4)
        nc.sync.dma_start(wt_halves[1][:], rows(wt, 1)[:, :, 2 * P :])
        load_plane(5)
        nc.sync.dma_start(wx_raw[:], rows(wx, 0))
        nc.sync.dma_start(c_early[1][:], rows(c, 0)[:, :, 512:])
        nc.sync.dma_start(c_early[0][:], rows(c, 0)[:, :, :128])
        load_plane(6)
        load_plane(7)
        nc.sync.dma_start(c_late[:], rows(c, 0)[:, :, LATE[0] : LATE[0] + LATE[1]])
        nc.sync.dma_start(bias[:], b.rearrange("(p t) -> p t", t=PACK))

        nc.vector.memset(warm[:, 0:1], 0.0)
        nc.scalar.activation(warm[:, 1:2], warm[:, 0:1], GELU)

        make_identity(nc, ident[:])
        eye = mx_tiles("eye", KP, 147)
        for i in range(PACK):
            eye_bf = place("eye_bf%d" % i, [P, KP], BF16, 72 + i)
            nc.vector.memset(eye_bf[:].bitcast(U32), 0)
            nc.vector.tensor_copy(eye_bf[:].rearrange("p (m i) -> p m i", i=PACK)[:, :, i], ident[:])
            quantize(eye, P * i, eye_bf[:])

        def dealt(w_bf):
            return w_bf.rearrange("p (t m i) -> p m i t", t=PACK, i=PACK)

        def by_slice(raw):
            return raw.rearrange("p i (m t) -> p m i t", t=PACK)

        def weave(copy, dst, src):
            copy(
                dst.rearrange("p (g r i) -> p g i r", r=4, i=PACK),
                src.rearrange("p i (g r) -> p g i r", r=4),
            )

        across = [bank_tile("across%d" % v, 6 + v) for v in range(2)]
        for s in range(PACK):
            nc.tensor.transpose(across[s // 2][:, P * (s % 2) : P * (s % 2 + 1)], wgt_rows[:, P * s : P * (s + 1)], ident[:])

        def repeat_quarter(q):
            h, v = q // 2, q % 2
            nc.scalar.copy(
                wgt_cols[q][:].rearrange("c (s g d r) -> c s g d r", s=2, g=GROUPS, d=2),
                across[v][:, : 2 * P].rearrange("c (s z g h d) -> c s z g h d", s=2, g=GROUPS, h=2, d=2)[:, :, 0, :, h, :].unsqueeze(4).to_broadcast([P, 2, GROUPS, 2, GROUPS]),
            )

        def spread_quarter(q):
            spread = bank_tile("spread%d" % q, 4 + q % 2)
            for s in range(2):
                nc.tensor.transpose(spread[:, P * s : P * (s + 1)], wgt_cols[q][:, P * s : P * (s + 1)], ident[:])
            nc.scalar.copy(wgt_sb[:, 2 * P * q : 2 * P * (q + 1)], spread[:, : 2 * P])

        repeat_quarter(0)
        for q in range(PACK):
            if q + 1 < PACK:
                repeat_quarter(q + 1)
            spread_quarter(q)

        wq0 = mx_tiles("wq0", N, 150)
        w_bf0 = place("w_bf0", [P, N * PACK], BF16, 69)
        for u in range(2):
            nc.vector.tensor_copy(dealt(w_bf0[:])[:, :, :, 2 * u : 2 * u + 2], by_slice(wt_raw[0][:])[:, :, :, 2 * u : 2 * u + 2])
        quantize(wq0, 0, w_bf0[:])
        wq = [wq0, mx_tiles("wq1", N, 152.5)]
        w_bf1 = [place("w_bf1_%d" % u, [P, 2 * N], BF16, 167.5 - 2 * u) for u in range(2)]

        def deal_half(copy, u, h):
            copy(
                w_bf1[u][:].rearrange("p (t m i) -> p m i t", t=2, i=PACK)[:, 64 * h : 64 * (h + 1)],
                by_slice(wt_halves[h][:])[:, :, :, 2 * u : 2 * u + 2],
            )

        minus_q = place("minus_q", [P, PACK * N], F32, 155)
        turned = place("turned", [P, N * PACK], BF16, 165)
        wr_bf = [place("wr_bf0", [P, N * PACK], BF16, 102), None]

        backs, sums = {}, {}

        def first_tier_back(a):
            for i in range(PACK):
                backs[a, i] = bank_tile("back%d_%d" % (a, i), i)
                matmul(backs[a, i][:], eye, P * i, wq[a], 0, True, True)

        def turn_weights(a, h):
            for nb in (2 * h, 2 * h + 1):
                sums[a, nb] = bank_tile("sum%d_%d" % (a, nb), PACK + nb)
                for i in range(PACK):
                    nc.tensor.matmul(sums[a, nb][:, P * i : P * (i + 1)], wt_raw[a][:, i, P * nb : P * (nb + 1)], ident[:],
                                     start=(i == 0), stop=False, is_transpose=True)

        def take_away(a, h):
            for i in range(PACK):
                at = N * i + 2 * P * h
                nc.scalar.activation(minus_q[:, at : at + 2 * P].rearrange("p (m t) -> p m t", t=PACK),
                                     backs[a, i][:].rearrange("p (t m) -> p m t", t=PACK)[:, 64 * h : 64 * (h + 1), :], COPY, scale=-1.0)
                for nb in (2 * h, 2 * h + 1):
                    nc.tensor.matmul(sums[a, nb][:, P * i : P * (i + 1)], minus_q[:, N * i + P * nb : N * i + P * (nb + 1)], ident[:],
                                     start=False, stop=(i == PACK - 1), is_transpose=True)

        def round_left(a, h):
            for nb in (2 * h, 2 * h + 1):
                nc.scalar.copy(turned[:, KP * nb : KP * (nb + 1)].rearrange("n (u p e) -> n u p e", u=2, e=2),
                               sums[a, nb][:].rearrange("n (u e p) -> n u p e", u=2, e=2))

        def turn_back(a, first_bank):
            for h in (1, 0):
                words = bank_tile("words%d_%d" % (a, h), first_bank + 1 - h)
                for nb2 in range(2):
                    for u in range(2):
                        at = 2 * P * (2 * h + nb2) + P * u
                        nc.tensor.transpose(words[:, P * (2 * nb2 + u) : P * (2 * nb2 + u + 1)], turned[:].bitcast(F32)[:, at : at + P], ident[:])
                nc.scalar.copy(
                    wr_bf[a][:].bitcast(F32).rearrange("p (t h b m u) -> p h t b m u", t=PACK, h=2, b=2, u=2)[:, h],
                    words[:].rearrange("p (b u m t) -> p t b m u", b=2, u=2, t=PACK),
                )

        first_tier_back(0)
        for h in (1, 0):
            turn_weights(0, h)
        for h in (1, 0):
            take_away(0, h)
        for h in (1, 0):
            round_left(0, h)
        turn_back(0, 0)
        for u in range(2):
            deal_half(nc.scalar.copy, u, 0)

        picked = [place("picked%d" % a, [P, PACK, J], F32, 72 + 16 * a) for a in range(2)]

        def pick(n, j0, width):
            nc.vector.tensor_tensor(
                picked[n // PACK][:, n % PACK, j0 : j0 + width],
                planes[n][:].indirect(offsets[:, j0 // 16 : (j0 + width) // 16]),
                wgt_sb[:, j0 : j0 + width],
                ALU.mult,
            )

        for q in range(PACK):
            pick(0, 2 * P * q, 2 * P)
        for n in range(1, PACK):
            pick(n, 0, J)
        wr = [(place("wr0_codes", [P, N], U32, 16), place("wr0_scales", [P, N], U8, 18)), mx_tiles("wr1", N, 64)]
        quantize(wr[0], 0, wr_bf[0][:])
        pick(4, 0, J)
        xg0_bf = [place("xg0_bf0", [P, HALF * PACK], BF16, 161.5), None]
        weave(nc.scalar.copy, xg0_bf[0][:, : PACK * 256], picked[0][:, :, :256])
        for u in range(2):
            deal_half(nc.scalar.copy, u, 1)
        quantize(wq[1], 0, w_bf1[0][:])
        xg0 = [(place("xg0a_codes", [P, HALF], U32, 155), place("xg0a_scales", [P, HALF], U8, 167.5)), None]
        quantize(xg0[0], 0, xg0_bf[0][:, : PACK * 256])
        quantize(wq[1], 2 * P, w_bf1[1][:])
        weave(nc.scalar.copy, xg0_bf[0][:, PACK * 256 :], picked[0][:, :, 256:HALF])
        quantize(xg0[0], 256, xg0_bf[0][:, PACK * 256 :])
        xg0_bf[1] = place("xg0_bf1", [P, HALF * PACK], BF16, 104)
        weave(nc.scalar.copy, xg0_bf[1][:], picked[0][:, :, HALF:])
        pick(5, 0, J)
        wr_bf[1] = place("wr_bf1", [P, N * PACK], BF16, 40)
        for q in range(4):
            u, h = q // 2, q % 2
            back = bank_tile("back1_%d" % q, (0, 7, 1, 2)[q])
            for i in range(PACK):
                for t2 in range(2):
                    col = (t2 * PACK + i) * 64
                    matmul(back[:, col : col + 64], eye, P * i, wq[1], P * (2 * u + t2) + 64 * h, True, True)
            nc.vector.tensor_tensor(
                dealt(wr_bf[1][:])[:, 64 * h : 64 * (h + 1), :, 2 * u : 2 * u + 2],
                by_slice(wt_halves[h][:])[:, :, :, 2 * u : 2 * u + 2],
                back[:].rearrange("p (t i m) -> p m i t", t=2, i=PACK),
                ALU.subtract,
            )
        ce_bf = [place("ce_bf0", [P, 128 * PACK], BF16, 191), place("ce_bf1", [P, HALF * PACK], BF16, 192)]
        for u in range(2):
            quantize(wr[1], 2 * P * u, wr_bf[1][:, 2 * N * u : 2 * N * (u + 1)])
        wx_bf = place("wx_bf", [P, N * PACK], BF16, 175)
        nc.scalar.copy(dealt(wx_bf[:]), by_slice(wx_raw[:]))
        weave(nc.scalar.copy, ce_bf[1][:], c_early[1][:])
        weave(nc.scalar.copy, ce_bf[0][:], c_early[0][:])
        xg1_bf = place("xg1_bf", [P, J * PACK], BF16, 120)

        def xg1_cols(j0, width):
            return xg1_bf[:, PACK * j0 : PACK * (j0 + width)]

        def weave_pair(copy, pair, j0, width):
            copy(
                xg1_cols(j0, width).rearrange("p (j i) -> p j i", i=PACK)[:, :, 2 * pair : 2 * pair + 2],
                picked[1][:, 2 * pair : 2 * pair + 2, j0 : j0 + width].rearrange("p i j -> p j i"),
            )

        on_s, on_v = nc.scalar.copy, nc.vector.tensor_copy
        for j0, width in EARLY + (LATE,):
            weave_pair(on_s, 0, j0, width)
        wxq = mx_tiles("wx", N, 160)
        quantize(wxq, 0, wx_bf[:])
        xg0[1] = (place("xg0b_codes", [P, HALF], U32, 157.5), place("xg0b_scales", [P, HALF], U8, 175))
        quantize(xg0[1], 0, xg0_bf[1][:])
        c_wide = mx_tiles("c_wide", HALF, 225)
        quantize(c_wide, 0, ce_bf[1][:])
        pick(6, 0, J)
        c_first = mx_tiles("c_first", 128, 224)
        quantize(c_first, 0, ce_bf[0][:])
        c_last = mx_tiles("c_last", 384, 179)

        acc = []
        first_bank = 0
        for j0, width in CHUNKS:
            nb = width * PACK // BANK
            acc.append([bank_tile("acc%d" % (first_bank + n), first_bank + n) for n in range(nb)])
            first_bank = first_bank + nb

        def passes(ci, pairs, opens, closes):
            width = CHUNKS[ci][1]
            per_bank = BANK // width
            for n, bank in enumerate(acc[ci]):
                for s, (lhs, rhs, col) in enumerate(pairs):
                    for r in range(per_bank):
                        t = n * per_bank + r
                        matmul(bank[:, r * width : (r + 1) * width], lhs, P * t, rhs, col,
                               opens and s == 0 and r == 0, closes and s == len(pairs) - 1 and r == per_bank - 1)

        for ci in (3, 0, 4, 2, 1):
            j0 = CHUNKS[ci][0]
            passes(ci, [(wq[0], xg0[j0 // HALF], j0 % HALF), (wr[0], xg0[j0 // HALF], j0 % HALF)], True, False)
        passes(0, [(wxq, c_first, 0)], False, False)
        for ci in (1, 2):
            passes(ci, [(wxq, c_wide, CHUNKS[ci][0] - HALF)], False, False)

        xg1 = mx_tiles("xg1", J, 181)
        yq = mx_tiles("y", J, 186)
        out_rows = out_0.rearrange("(p t) j -> p t j", t=PACK)
        out_words = out_1[0].rearrange("p j i -> p (j i)").bitcast(I32)

        def finish_sum(ci, copy):
            j0, width = CHUNKS[ci]
            weave_pair(copy, 1, j0, width)
            quantize(xg1, j0, xg1_cols(j0, width))
            passes(ci, [(wq[1], xg1, j0), (wr[1], xg1, j0)], False, True)

        y_bf = place("y_bf", [P, J * PACK], BF16, 204)
        ys = {}

        def activate(ci, copy):
            j0, width = CHUNKS[ci]
            y = place("y%d" % ci, [P, PACK, width], F32, (0, 4, 8, 12, 24)[ci])
            per_bank = BANK // width
            for t in range(PACK):
                r = t % per_bank
                nc.scalar.activation(y[:, t, :], acc[ci][t // per_bank][:, r * width : (r + 1) * width], GELU, bias=bias[:, t : t + 1])
                if r == per_bank - 1:
                    nc.sync.dma_start(out_rows[:, t - r : t + 1, j0 : j0 + width], y[:, t - r : t + 1, :])
            ys[ci] = y
            if copy is not None:
                weave_y(ci, copy)

        def weave_y(ci, copy):
            j0, width = CHUNKS[ci]
            weave(copy, y_bf[:, PACK * j0 : PACK * (j0 + width)], ys[ci][:])

        def quantize_y(j0, j1):
            quantize(yq, j0, y_bf[:, PACK * j0 : PACK * j1])

        def store_words(j0, j1):
            nc.sync.dma_start(out_words[:, j0:j1], yq[0][:, j0:j1].bitcast(I32))

        pick(7, *CHUNKS[0])
        finish_sum(0, on_v)
        pick(7, *CHUNKS[1])
        finish_sum(1, on_s)
        pick(7, *CHUNKS[2])
        finish_sum(2, on_s)
        pick(7, *LATE)
        cl_bf = place("cl_bf", [P, 384 * PACK], BF16, 196)
        weave(on_v, cl_bf[:], c_late[:])
        quantize(c_last, 128, cl_bf[:, PACK * 128 :])
        quantize(c_last, 0, cl_bf[:, : PACK * 128])
        passes(3, [(wxq, c_last, 128)], False, False)
        passes(4, [(wxq, c_last, 0)], False, False)
        finish_sum(3, on_v)
        finish_sum(4, on_v)
        activate(0, None)
        activate(1, on_v)
        activate(2, on_v)
        quantize_y(512, 1024)
        activate(3, on_v)
        store_words(512, 1024)
        quantize_y(256, 512)
        activate(4, None)
        weave_y(0, on_s)
        quantize_y(0, 128)
        weave_y(4, on_v)
        quantize_y(128, 256)
        store_words(0, 512)
        for q in range(4):
            queue = nc.sync if q % 2 == 0 else nc.scalar
            queue.dma_start(out_2[0, 4 * q : 4 * q + 4, :].bitcast(I32), yq[1][32 * q : 32 * q + 4, :].bitcast(I32))
